import numpy as np, ml_dtypes
CORES = [2,42,66,74,82,90,114]
N = 7
import mx_ref
BF = ml_dtypes.bfloat16
def entries(a):
    return np.ascontiguousarray(a.T).reshape(-1)
def table(e):
    return np.ascontiguousarray(np.reshape(e, (-1, 16)).T).astype(np.int32)
def cols(t, e):
    v = np.concatenate([t.reshape(128, -1, 4), np.zeros((128, 1, 4), BF)], axis=1)
    return np.ascontiguousarray(v[:, e]).reshape(128, -1)
def cut(t, i, w=512):
    return t[:, w * i:w * i + w]
def f(rng, *shape):
    return mx_ref.flush((rng.standard_normal(shape, dtype=np.float32) * np.exp2(rng.integers(-2, 3, shape[:-1] + (1,)))).astype(BF))
def wide(rng, *shape, cols=0):
    v = rng.standard_normal(shape, dtype=np.float32) * np.exp2(rng.integers(-12, 13, shape)).astype(np.float32)
    if cols: v *= np.repeat(np.exp2(rng.integers(-cols, cols + 1, shape[:-2] + (1, shape[-1] // 4))) * (rng.random(shape[:-2] + (1, shape[-1] // 4)) > 0.0625), 4, axis=-1).astype(np.float32)
    return mx_ref.flush(v.astype(BF))
T, O = 256, 1
def places(rng, dest):
    e = np.zeros((N, T), int)
    for d in range(N): e[dest == d] = d * T + rng.permutation(T)
    return np.stack([table(e[r]) for r in range(N)])
def relabel(rng):
    p = rng.permutation(N)
    if np.all((p - np.arange(N)) % N == p[0]): p[[0, 1]] = p[[1, 0]]
    return p
def setup_inputs(rng):
    e = rng.permutation(N * T).reshape(N, T)
    return {"x": f(rng, N, 128, 4 * T), "to": np.stack([table(e[r]) for r in range(N)]), "w": f(rng, N, 128, 512 * O)}
def setup_inputs_swap(rng):
    d = setup_inputs(rng); p = rng.permutation(N); dest = np.zeros((N, T), int)
    for k in range(N): dest[p[k]] = p[(k + 1) % N]
    d["to"] = places(rng, dest); return d
def setup_inputs_ones(rng):
    d = setup_inputs(rng); i = np.arange(N); n = np.ones((N, N), int); n[i, rng.permutation(N)] += T % N
    for t in range(T // N - 1): n[i, rng.permutation(N)] += N
    d["to"] = places(rng, np.stack([rng.permutation(np.repeat(i, n[r])) for r in range(N)])); return d
def setup_inputs_runs(rng):
    d = setup_inputs(rng); p = relabel(rng); s, u = rng.integers(1, N), rng.integers(0, N); g, h = rng.permutation(N), rng.permutation(N)
    n = T // N + ((g[:, None] + h) % N < T % N)
    j = (np.arange(N) + s * np.arange(N)[:, None] + u) % N
    d["to"] = places(rng, np.stack([np.repeat(p[j[r]], n[r, j[r]]) for r in range(N)])); return d
def setup_inputs_comb(rng):
    d = setup_inputs(rng); p = relabel(rng); s, u = rng.integers(1, N), rng.integers(0, N); k = rng.permutation(N); c = np.arange(T)
    d["to"] = places(rng, np.stack([p[(c + np.where(c < T - T % N, s * r + u, k[r])) % N] for r in range(N)])); return d
def setup_inputs_spread(rng):
    d = setup_inputs(rng); d["x"] = wide(rng, N, 128, 4 * T, cols=8); return d
def check_inputs(d):
    e = np.concatenate([entries(d["to"][r]) for r in range(N)])
    return [] if np.array_equal(np.sort(e), np.arange(N * T)) else ["to"]
def reference(x, to, w):
    z = np.concatenate([x[r] for r in range(N)], axis=1)
    e = np.concatenate([entries(to[r]) for r in range(N)])
    home = np.zeros(N * T, int); home[e] = np.arange(N * T)
    y = np.zeros((N, 128, O * T), np.float32)
    for d in range(N):
        v = mx_ref.quantize(cols(z, home[d * T:d * T + T]))
        for o in range(O): y[d][:, T * o:T * o + T] = mx_ref.matmul(mx_ref.quantize(np.ascontiguousarray(cut(w[d], o))), v)
    return {"y": y}

@@ -1,0 +1,305 @@
+from concourse.bass import DstId, RemoteDMATransfer
+from concourse.mybir import dt, AluOpType, ActivationFunctionType
+
+N, C = 7, 256
+P1, P2, S2 = 37, 42, 48
+L1W = 48 + 6 * P1
+U = 1024
+CA = 352
+R23 = 12582912.0
+
+F32, BF, I32, U16, CODES, PLANE = "float32", "bfloat16", "int32", "uint16", "float8_e4m3fn_x4", "uint8"
+SCRATCH = {
+    "ta": ("sbuf", [128, 33], F32), "td3": ("sbuf", [128, 32], F32),
+    "tb": ("sbuf", [128, 65], F32), "tdb": ("sbuf", [128, 64], F32), "tdc": ("sbuf", [128, 32], F32),
+    "ic": ("sbuf", [128, 32], F32), "win": ("sbuf", [128, 16], BF), "win2": ("sbuf", [128, 16], BF),
+    "wme": ("sbuf", [128, 16], BF), "rst": ("sbuf", [128, C], BF), "rst7": ("sbuf", [128, 7 * 32], F32),
+    "cv": ("sbuf", [128, 128], F32), "cvb": ("sbuf", [128, 128], BF),
+    "ji": ("sbuf", [128, 34], F32), "jm": ("sbuf", [128, 34], I32), "jf": ("sbuf", [128, 34], F32),
+    "ja": ("sbuf", [128, 34], F32), "jb": ("sbuf", [128, 34], F32), "jc": ("sbuf", [128, 34], F32),
+    "sig": ("sbuf", [128, 34], U16), "dup": ("sbuf", [128, 32], U16), "pos": ("sbuf", [128, 32], F32),
+    "qc": ("sbuf", [128, 8], F32), "ba": ("sbuf", [128, 8], F32), "zr": ("sbuf", [128, 8], F32),
+    "mg": ("sbuf", [128, 8], F32),
+    "tw": ("sbuf", [128, 16], I32), "td16": ("sbuf", [128, 16], U16),
+    "mk": ("sbuf", [128, C], BF), "jk": ("sbuf", [128, C], BF), "jn": ("sbuf", [128, C], F32),
+    "dm": ("sbuf", [128, C], BF), "cc": ("sbuf", [128, C], BF),
+    "xx": ("sbuf", [128, C], BF), "xc": ("sbuf", [128, C], BF),
+    "s16": ("sbuf", [128, 8], U16), "inv": ("sbuf", [128, 272], BF), "gg": ("sbuf", [128, 544], BF),
+    "yy": ("sbuf", [128, 544], BF), "lf": ("sbuf", [128, 18], F32), "lst1": ("sbuf", [128, 18], U16),
+    "cb": ("sbuf", [128, 4 * N], F32), "c7": ("sbuf", [128, 8], F32),
+    "zz": ("sbuf", [128, 48], F32),
+    "qa": ("sbuf", [128, 8], F32), "qi": ("sbuf", [128, 8], I32),
+    "aa": ("sbuf", [128, 8], F32), "jj": ("sbuf", [128, 8], F32),
+    "gr": ("sbuf", [128, 7 * 32], F32), "gs": ("sbuf", [128, 7 * 32], F32),
+    "l2t": ("sbuf", [128, 32], F32), "lst2": ("sbuf", [128, 22], U16),
+    "rd": ("dram", [128, 2], I32), "lr": ("dram", [N, 128, 2], I32),
+    "tr": ("sbuf", [128, 16], I32), "tr16": ("sbuf", [128, 16], U16),
+    "trd16": ("sbuf", [128, 16], U16), "mk3": ("sbuf", [128, C], BF), "kv": ("sbuf", [128, C], BF),
+    "vw": ("sbuf", [128, N * C], BF), "vl": ("sbuf", [128, C], BF),
+    "f1": ("sbuf", [128, 8], F32), "f2": ("sbuf", [128, 8], F32),
+    "ft": ("sbuf", [128, 32], F32), "w3": ("sbuf", [128, 512], F32), "y3": ("sbuf", [128, 512], F32),
+    "fa": ("sbuf", [128, 64], F32), "fb": ("sbuf", [128, 32], F32), "pk": ("sbuf", [128, 16], I32),
+    "ql": ("sbuf", [128, 16], I32), "qh": ("sbuf", [128, 16], I32), "qq": ("sbuf", [128, 16], I32),
+    "ua": ("sbuf", [128, 16], F32), "ub": ("sbuf", [128, 16], F32),
+    "uc": ("sbuf", [128, 16], F32), "ud": ("sbuf", [128, 16], F32), "lst3": ("sbuf", [128, 16], U16),
+    "xt": ("sbuf", [128, 4 * C], BF), "wt": ("sbuf", [128, 512], BF),
+    "xq": ("sbuf", [128, C], CODES), "xs": ("sbuf", [128, C], PLANE),
+    "wq": ("sbuf", [128, 128], CODES), "ws": ("sbuf", [128, 128], PLANE),
+    "out1q": ("sbuf", [128, 240], CODES), "out1s": ("sbuf", [128, 240], PLANE),
+    "land1q": ("sbuf", [128, L1W], CODES), "land1s": ("sbuf", [128, L1W], PLANE),
+    "out2q": ("sbuf", [128, 6 * S2], CODES), "out2s": ("sbuf", [128, 6 * S2], PLANE),
+    "land2q": ("sbuf", [128, 7 * S2], CODES), "land2s": ("sbuf", [128, 7 * S2], PLANE),
+    "fq": ("sbuf", [128, C], CODES), "fs": ("sbuf", [128, C], PLANE),
+    "ps": ("psum", [128, 1024], F32), "ys": ("sbuf", [128, C], F32),
+}
+SEMAPHORES = ["ev", "es", "eg", "et",
+              "d_rd", "d_tw", "d_x", "d_w", "d_own", "d_tr", "d_vl", "d_y0", "d_y1",
+              "a_raw", "a_cnt", "a_c1", "a_s1", "a_c2", "a_s2",
+              "l_raw", "l_cnt", "l_c1", "l_s1", "l_c2", "l_s2"]
+
+
+def rank_program(g, core, T, topo):
+    me = T.rank_of(core)
+    if me is None:
+        return
+    A, AF = AluOpType, ActivationFunctionType
+    queue = {"v": g.vector, "s": g.scalar, "g": g, "t": g.tensor, "y": g.sync}
+    count = {}
+    seen = {k: {} for k in queue}
+
+    def wait(q, *deps):
+        for sem, n in deps:
+            if seen[q].get(sem, 0) < n:
+                queue[q].wait_ge(T.sem[sem], n)
+                seen[q][sem] = n
+
+    def op(q, call, *deps):
+        wait(q, *deps)
+        sem = "e" + q
+        call().then_inc(T.sem[sem], 1)
+        count[sem] = count.get(sem, 0) + 1
+        return (sem, count[sem])
+
+    def dma(q, sem, out, in_, *deps):
+        wait(q, *deps)
+        queue[q].dma_start(out, in_).then_inc(T.sem[sem], 16)
+        count[sem] = count.get(sem, 0) + 16
+        return (sem, count[sem])
+
+    V, S = g.vector, g.scalar
+
+    peers = [T.cores[(me + 1 + x) % N] for x in range(N - 1)]
+    eng = [e for e in topo.engines(core, peers[0]) if all(e in topo.engines(core, p) for p in peers)]
+    ev, od = eng[0::2], eng[1::2]
+
+    def mask(es):
+        return sum(1 << e for e in es)
+
+    one = [[e] for e in ev] + [od[0:2], od[2:4]]
+    two = [ev[0:2], ev[2:4]] + [[e] for e in od]
+
+    def dst(p):
+        rid, pid, _ = topo.addr(p)
+        return DstId(rid=rid, pnc=pid)
+
+    def to_all(src, d, es, remote, local):
+        g.remote_dma_fused([RemoteDMATransfer(dst_ids=[dst(p) for p in peers], dma_engine_mask=mask(es),
+                                              remote_sem=T.sem[remote], srcs=[src], dsts=[d] * len(peers))],
+                           local_sem=T.sem[local])
+
+    def to_each(srcs, dsts, masks, remote, local):
+        g.remote_dma_fused([RemoteDMATransfer(dst_ids=[dst(p)], dma_engine_mask=mask(m), remote_sem=T.sem[remote],
+                                              src=s, dst=d) for p, s, d, m in zip(peers, srcs, dsts, masks)],
+                           local_sem=T.sem[local])
+
+    rd = dma("y", "d_rd", T.rd[:], T.to[:])
+    for i in range(8):
+        tw = dma("sy"[i % 2], "d_tw", T.tw[16 * i:16 * i + 16, :], T.to[:])
+    xl = dma("y", "d_x", T.xt[:], T.x[:])
+    own = dma("s", "d_own", T.lr[me], T.to[:])
+    wl = dma("s", "d_w", T.wt[:], T.w[:])
+
+    flag = dict(allow_small_or_imprecise_dtypes=True)
+    k_ta = op("g", lambda: g.iota(T.ta[:], [[1, 11], [0, 3]], 0, 0, **flag))
+    k_ic = op("g", lambda: g.iota(T.ic[:], [[0, 2], [1, 16]], 0, 0, **flag))
+    k_ji = op("g", lambda: g.iota(T.ji[:], [[16, 17], [0, 2]], 0, 0, **flag))
+    k_tb = op("g", lambda: g.iota(T.tb[:, 0:32], [[16, 2], [0, 16]], 0, 0, **flag))
+    k_cv = op("g", lambda: g.iota(T.cv[:], [[32, 8], [1, 16]], 0, 0, **flag))
+    wait("g", rd)
+    raw = eng[:1]
+    to_all(T.rd[:], T.lr[me], raw, "a_raw", "l_raw")
+    k_tc = op("g", lambda: g.iota(T.tb[:, 32:65], [[0, 11], [16, 3]], 0, 0, **flag))
+
+    op("v", lambda: V.memset(T.dm[:, 0:1], -255.0))
+    k_rst = op("v", lambda: V.memset(T.rst[:], 1.0))
+    k_inv = op("v", lambda: V.memset(T.inv[:], 0.0))
+    k_td3 = op("v", lambda: V.transpose(T.td3[:], T.ta[:, 0:32]), k_ta)
+    k_mem = op("v", lambda: V.memset(T.rst[:, 0:C:32], 0.0), k_rst)
+    pd, p15, odd, pr = T.td3[:, 0:1], T.tdc[:, 0:1], T.tdb[:, 0:1], T.tdb[:, 32:33]
+    k_win2 = op("v", lambda: V.tensor_scalar(T.win2[:], T.ic[:, 0:16], pd, None, A.is_lt), k_td3, k_ic)
+    k_win = op("v", lambda: V.tensor_scalar(T.win[:], T.ic[:, 0:16], pd, 256.0, A.is_equal, A.mult))
+    k_tdc = op("v", lambda: V.transpose(T.tdc[:], T.ic[:]))
+    k_wme = op("v", lambda: V.tensor_scalar(T.wme[:], T.ic[:, 0:16], float(me), None, A.is_equal))
+    k_tdb = op("v", lambda: V.transpose(T.tdb[:, 0:32], T.tb[:, 0:32]), k_tb)
+    k_jf = op("s", lambda: S.activation(T.jf[:], T.ji[:], AF.Identity, bias=p15), k_tdc, k_ji)
+    k_jm = op("v", lambda: V.tensor_scalar(T.jm[:], T.jf[:], -18.0, 1.0 / P1, A.add, A.mult), k_jf)
+    k_ja = op("s", lambda: S.activation(T.ja[:], T.jf[:], AF.Identity, bias=1.0, scale=7.0), k_jf)
+
+    k_td = op("v", lambda: V.tensor_scalar(T.td16[:], T.tw[:], -127.5, 1.0 / C, A.add, A.mult), tw)
+    bm, nm = T.cb[:, 4 * me:4 * me + 1], T.cb[:, 4 * me + 1:4 * me + 2]
+    k_b = op("s", lambda: S.activation(T.jk[:], T.win2[:].indirect(T.td16[:]), AF.Identity, accum_out=bm), k_td, k_win2)
+    k_jb = op("v", lambda: V.tensor_scalar(T.jb[:], T.jm[:], float(1 - 7 * P1), None, A.mult), k_jm)
+    k_mk = op("v", lambda: V.tensor_copy(T.mk[:], T.win[:].indirect(T.td16[:])), k_td, k_win)
+    k_nm = op("s", lambda: S.activation(T.jn[:], T.mk[:], AF.Identity, bias=3.0 / 7 / C, scale=1.0 / 7 / 256,
+                                        accum_out=nm), k_mk)
+    k_jc = op("v", lambda: V.tensor_tensor(T.jc[:], T.ja[:], T.jb[:], A.add), k_jb, k_ja)
+    k_dm = op("v", lambda: V.tensor_scalar(T.dm[:, 1:C], T.mk[:, 0:C - 1], -255.0 / 256, None, A.mult), k_mk)
+    k_sig = op("v", lambda: V.tensor_copy(T.sig[:], T.jc[:]), k_jc)
+    k_cc = op("v", lambda: V.tensor_tensor_scan(T.cc[:], T.mk[:], T.dm[:], bm, A.add, A.add), k_dm, k_b)
+    k_xx = op("v", lambda: V.transpose(T.xx[:], T.cc[:]), k_cc)
+    k_xc = op("v", lambda: V.tensor_tensor_scan(T.xc[:], T.rst[:], T.xx[:], 0.0, A.mult, A.max), k_xx, k_mem)
+    k_s = op("v", lambda: V.tensor_copy(T.s16[:], T.xc[:, 31:C:32]), k_xc)
+    k_cvb = op("s", lambda: S.activation(T.cvb[:], T.cv[:], AF.Identity, bias=odd), k_cv, k_tdb)
+    k_sc = op("v", lambda: V.tensor_copy(T.inv[:].indirect(T.s16[:]), T.cvb[:]), k_s, k_cvb, k_inv)
+
+    def lin(out, a, b, scale, bias):
+        return op("s", lambda: S.activation(out[:, a:b], T.ic[:, a:b], AF.Identity, bias=float(bias), scale=float(scale)),
+                  k_ic)
+
+    fp, rx, aj = T.zz[:, 0:32], 32, 40
+    k_zz = op("s", lambda: S.activation(T.zz[:], T.cv[:, 0:48], AF.Copy, scale=0.0))
+    k_mg = lin(T.mg, 0, 8, 0, -R23)
+    op("s", lambda: S.activation(T.rst7[:, 0:128], T.cv[:], AF.Identity, bias=1.0, scale=0.0))
+    k_r7 = op("s", lambda: S.activation(T.rst7[:, 128:224], T.cv[:, 0:96], AF.Identity, bias=1.0, scale=0.0))
+    k_r7 = op("s", lambda: S.activation(T.rst7[:, 0:224:7], T.cv[:, 0:32], AF.Copy, scale=0.0), k_r7)
+
+    k_ga = op("s", lambda: S.activation(T.gg[:, 0:CA], T.inv[:].indirect(T.sig[:, 0:CA // 16]), AF.Copy), k_sc, k_sig)
+    k_gb = op("v", lambda: V.tensor_copy(T.gg[:, CA:544], T.inv[:].indirect(T.sig[:, CA // 16:34])), k_sc, k_sig)
+    k_xq = op("v", lambda: V.quantize_mx(T.xq[:], T.xs[:], T.xt[:]), xl)
+    k_yy = op("v", lambda: V.transpose(T.yy[:], T.gg[:]), k_ga, k_gb)
+    k_lf = op("v", lambda: V.tensor_tensor(T.lf[:, 0:17], T.yy[:, 0:544:32], T.yy[:, 16:544:32], A.add), k_yy)
+    k_l1 = op("v", lambda: V.tensor_copy(T.lst1[:, 0:17], T.lf[:, 0:17]), k_lf)
+    k_qc = lin(T.qc, 0, me + 1, 1, 3 - me)
+    if me < N - 1:
+        k_qc = lin(T.qc, me + 1, N, 1, 3 - me - N)
+
+    wait("g", k_nm)
+    to_all(T.cb[:, 4 * me:4 * me + 2], T.cb[:, 4 * me:4 * me + 2], eng, "a_cnt", "l_cnt")
+
+    lo, la = T.lst1[:, 2:17], T.lst1[:, 0:3]
+    u32, u8 = dt.uint32, dt.uint8
+    k_p1 = op("v", lambda: V.tensor_copy(T.out1q[:].bitcast(u32), T.xq[:].bitcast(u32).indirect(lo)), k_l1, k_xq)
+    k_o1 = op("s", lambda: S.activation(T.out1s[:], T.xs[:].indirect(lo), AF.Copy), k_l1, k_xq)
+    wait("g", k_p1)
+    blk = [P1 * (x + 1) - 32 for x in range(N - 1)]
+    lnd = [48 + P1 * x for x in range(N - 1)]
+    to_each([T.out1q[:, a:a + P1].bitcast(u8) for a in blk], [T.land1q[:, a:a + P1].bitcast(u8) for a in lnd], one,
+            "a_c1", "l_c1")
+    wait("g", k_o1)
+    to_each([T.out1s[:, a:a + P1] for a in blk], [T.land1s[:, a:a + P1] for a in lnd], two, "a_s1", "l_s1")
+    k_a1 = op("v", lambda: V.tensor_copy(T.land1q[:, 0:48].bitcast(u32), T.xq[:].bitcast(u32).indirect(la)))
+    k_tdd = op("v", lambda: V.transpose(T.tdb[:, 32:64], T.tb[:, 32:64]), k_tc)
+    k_b1 = op("s", lambda: S.activation(T.land1s[:, 0:48], T.xs[:].indirect(la), AF.Copy))
+
+    k_vl = op("g", lambda: g.iota(T.vl[:], [[0, C]], 0, 0, **flag))
+
+    dma("y", "d_tr", T.tr[112:128, :], T.to[:])
+    tr = dma("y", "d_tr", T.tr[0:112, :], T.lr[:], own, ("a_raw", 6 * len(raw)))
+
+    k_pos = op("s", lambda: S.activation(T.pos[:], T.ic[:], AF.Identity, bias=pr), k_tdd)
+    if me < N - 1:
+        lin(T.ba, me + 1, N, -P1, 48 - P1 + P1 * (me + N))
+    if me > 0:
+        lin(T.ba, 0, me, -P1, 48 - P1 + P1 * me)
+    k_ba = lin(T.ba, me, me + 1, 0, 0)
+    k_vw = op("s", lambda: S.activation(T.vw[:, C * me:C * me + C], T.rst[:], AF.Identity, bias=-4096.0, scale=0.0),
+              k_mem)
+
+    bb, nn = T.cb[:, 0:4 * N:4], T.cb[:, 1:4 * N:4]
+    cn = ("a_cnt", 6 * len(eng))
+    k_c7 = op("v", lambda: V.tensor_scalar(T.c7[:, 0:N], nn, R23, None, A.add), cn, k_nm)
+    k_q = op("v", lambda: V.tensor_tensor(T.qa[:, 0:N], bb, T.qc[:, 0:N], A.add), k_qc, k_b)
+    k_rx = op("v", lambda: V.tensor_tensor_scan(T.zz[:, rx + 1:rx + 8], T.c7[:, 0:N], T.mg[:, 0:N], 0.0, A.add, A.add),
+              k_c7, k_mg, k_zz)
+    k_qi = op("v", lambda: V.tensor_scalar(T.qi[:, 0:N], T.qa[:, 0:N], 1.0 / 7, None, A.mult), k_q)
+    k_aa = op("v", lambda: V.tensor_tensor(T.aa[:, 0:N], T.qi[:, 0:N], T.ba[:, 0:N], A.add), k_qi, k_ba)
+    kb = op("v", lambda: V.tensor_copy(T.tr16[:], T.tr[:]), tr)
+    k_a = op("v", lambda: V.tensor_tensor(T.zz[:, aj + 1:aj + 8], T.aa[:, 0:N], T.zz[:, rx:rx + N], A.subtract),
+             k_rx, k_aa)
+    k_t3 = op("v", lambda: V.tensor_scalar(T.trd16[:], T.tr[:], -127.5, 1.0 / C, A.add, A.mult))
+    k_jj = op("v", lambda: V.tensor_tensor(T.jj[:, 0:N], T.zz[:, aj + 1:aj + 8], T.zz[:, aj:aj + N], A.subtract), k_a)
+    k_mk3 = op("s", lambda: S.activation(T.mk3[:], T.wme[:].indirect(T.trd16[:]), AF.Copy), k_t3, k_wme)
+    k_zr = lin(T.zr, 0, N, 1, 12 - me)
+    k_gr = op("v", lambda: V.tensor_scalar(T.gr[:, 0:224:7], T.pos[:], T.jj[:, 0:1], None, A.add), k_jj, k_pos)
+    for r in range(1, N):
+        k_gr = op("v", lambda: V.tensor_scalar(T.gr[:, r:224:7], T.pos[:], T.zz[:, rx + r:rx + r + 1], T.jj[:, r:r + 1],
+                                               A.is_ge, A.mult))
+    k = op("v", lambda: V.tensor_tensor_scan(T.gs[:], T.rst7[:], T.gr[:], 0.0, A.mult, A.add), k_gr, k_r7)
+    k = op("v", lambda: V.transpose(T.l2t[:], T.gs[:, 6:224:7]), k)
+    e = 3 * (N - 1 - me)
+    if e:
+        op("v", lambda: V.tensor_scalar(T.lst2[:, 0:e], T.l2t[:, 3 * (me + 1):21], float(L1W - 1), None, A.min), k)
+    k_l2 = op("v", lambda: V.tensor_scalar(T.lst2[:, e:21], T.l2t[:, 0:3 * (me + 1)], float(L1W - 1), None, A.min), k)
+
+    k = op("v", lambda: V.tensor_tensor_scan(T.kv[:], T.mk3[:], T.mk3[:], 0.0, A.add, A.max), k_mk3)
+    k_v = op("v", lambda: V.tensor_copy(T.vw[:].indirect(T.tr16[:]), T.kv[:]), k, kb, k_vw)
+    for i in range(4):
+        vl = dma("y", "d_vl", T.vl[32 * i:32 * i + 4 * N:4, :], T.vw[0:16 * N:16, C * me:C * me + C], k_v, k_vl)
+
+    lo, la = T.lst2[:, 0:18], T.lst2[:, 18:21]
+    c1, s1 = ("a_c1", 8), ("a_s1", 8)
+    k_p2 = op("v", lambda: V.tensor_copy(T.out2q[:].bitcast(u32), T.land1q[:].bitcast(u32).indirect(lo)),
+              k_l2, k_a1, c1)
+    k_o2 = op("s", lambda: S.activation(T.out2s[:], T.land1s[:].indirect(lo), AF.Copy), k_l2, k_b1, s1)
+    wait("g", k_p2)
+    blk = [S2 * x for x in range(N - 1)]
+    lnd = [S2 * (N - 2 - x) for x in range(N - 1)]
+    to_each([T.out2q[:, a:a + P2].bitcast(u8) for a in blk], [T.land2q[:, a:a + P2].bitcast(u8) for a in lnd], one,
+            "a_c2", "l_c2")
+    wait("g", k_o2)
+    to_each([T.out2s[:, a:a + P2] for a in blk], [T.land2s[:, a:a + P2] for a in lnd], two, "a_s2", "l_s2")
+    k_a2 = op("v", lambda: V.tensor_copy(T.land2q[:, 6 * S2:7 * S2].bitcast(u32),
+                                         T.land1q[:].bitcast(u32).indirect(la)))
+    k_f1 = op("v", lambda: V.tensor_tensor(T.f1[:, 0:N], bb, T.zr[:, 0:N], A.add), k_zr)
+    k_f2 = op("v", lambda: V.tensor_scalar(T.f2[:, 0:N], T.zz[:, rx:rx + N], 7.0 * U, -1.0 * U, A.mult, A.add))
+    k_f = op("v", lambda: V.tensor_tensor(T.zz[:, 0:4 * N:4], T.f1[:, 0:N], T.f2[:, 0:N], A.add), k_f2)
+    k_dup = op("v", lambda: V.tensor_copy(T.dup[:], T.jf[:, 0:32]))
+    k_ft = op("v", lambda: V.transpose(T.ft[:], fp), k_f)
+    k_wq = op("v", lambda: V.quantize_mx(T.wq[:], T.ws[:], T.wt[:]), wl)
+
+    for i in range(2):
+        h = slice(256 * i, 256 * i + 256)
+        k = op("s", lambda: S.activation(T.w3[:, h], T.vl[:].indirect(T.dup[:, 16 * i:16 * i + 16]), AF.Relu,
+                                         bias=T.ft[:, 3 * me:3 * me + 1], scale=float(U + 1)), vl, k_ft, k_dup)
+        k = op("v", lambda: V.transpose(T.y3[:, h], T.w3[:, h]), k)
+    k_b2 = op("s", lambda: S.activation(T.land2s[:, 6 * S2:7 * S2], T.land1s[:].indirect(la), AF.Copy))
+    k = op("v", lambda: V.tensor_tensor(T.fa[:], T.y3[:, 0:512:8], T.y3[:, 4:512:8], A.add), k)
+    k = op("v", lambda: V.tensor_tensor(T.fb[:], T.fa[:, 0:64:2], T.fa[:, 1:64:2], A.add), k)
+    k = op("v", lambda: V.tensor_tensor(T.pk[:], T.fb[:, 0:32:2], T.fb[:, 1:32:2], A.add), k)
+    kl = op("v", lambda: V.tensor_scalar(T.ql[:], T.pk[:], U - 1, None, A.bitwise_and), k)
+    kh = op("v", lambda: V.tensor_scalar(T.qh[:], T.pk[:], 0.5 - 3.5 * U, 1.0 / (7 * U), A.add, A.mult))
+    kq = op("v", lambda: V.tensor_scalar(T.qq[:], T.ql[:], -3.0, 1.0 / 7, A.add, A.mult), kl)
+    ka = op("v", lambda: V.tensor_scalar(T.ua[:], T.ql[:], float(S2), None, A.mult))
+    kb = op("v", lambda: V.tensor_scalar(T.ub[:], T.qq[:], -7.0 * S2, None, A.mult), kq)
+    kc = op("v", lambda: V.tensor_tensor(T.uc[:], T.ua[:], T.qh[:], A.add), ka, kh)
+    kd = op("v", lambda: V.tensor_tensor(T.ud[:], T.ub[:], T.uc[:], A.add), kb, kc)
+    k_l3 = op("v", lambda: V.tensor_copy(T.lst3[:], T.ud[:]), kd)
+
+    c2, s2 = ("a_c2", 8), ("a_s2", 8)
+    cols = [slice(128 * i, 128 * i + 128) for i in range(2)]
+    lst = [T.lst3[:, 8 * i:8 * i + 8] for i in range(2)]
+    kq = [op("v", lambda: V.tensor_copy(T.fq[:, cols[i]].bitcast(u32), T.land2q[:].bitcast(u32).indirect(lst[i])),
+             k_l3, k_a2, c2) for i in range(2)]
+    ks = [op("s", lambda: S.activation(T.fs[:, cols[0]], T.land2s[:].indirect(lst[0]), AF.Copy), k_l3, k_b2, s2),
+          op("v", lambda: V.tensor_copy(T.fs[:, cols[1]], T.land2s[:].indirect(lst[1])), k_b2, s2)]
+    mm = [op("t", lambda: g.tensor.matmul_mx(T.ps[:, 512 * i:512 * i + 128], T.wq[:], T.ws[:], T.fq[:, cols[i]],
+                                             T.fs[:, cols[i]], True, True), kq[i], ks[i], k_wq) for i in range(2)]
+    k0 = op("s", lambda: S.activation(T.ys[:, 0:128], T.ps[:, 0:128], AF.Copy), mm[0])
+    k1 = op("v", lambda: V.tensor_copy(T.ys[:, 128:256], T.ps[:, 512:640]), mm[1])
+    y0 = dma("s", "d_y0", T.y[:, 0:128], T.ys[:, 0:128], k0)
+    y1 = dma("y", "d_y1", T.y[:, 128:256], T.ys[:, 128:256], k1)
+
+    wait("g", ("l_raw", len(raw)))
+    for sem in ("l_cnt", "l_c1", "l_s1", "l_c2", "l_s2"):
+        wait("g", (sem, len(eng)))
+    wait("y", y0, y1, *[(s, count[s]) for s in ("ev", "es", "eg", "et")])

@@ -3,65 +3,129 @@ from concourse.mybir import dt, AluOpType, ActivationFunctionType
 
 N, C = 7, 256
 P1, P2, S2 = 37, 42, 48
-L1W = 48 + 6 * P1
-U = 1024
-CA = 352
+OWN1 = 112
+L1W = OWN1 + 48 + 3 * P1
+U = 4096
+SHIFT = 7 * U - 13300
+CA = 288
 R23 = 12582912.0
 
 F32, BF, I32, U16, CODES, PLANE = "float32", "bfloat16", "int32", "uint16", "float8_e4m3fn_x4", "uint8"
 SCRATCH = {
     "ta": ("sbuf", [128, 33], F32), "td3": ("sbuf", [128, 32], F32),
-    "tb": ("sbuf", [128, 65], F32), "tdb": ("sbuf", [128, 64], F32), "tdc": ("sbuf", [128, 32], F32),
+    "tb": ("sbuf", [128, 32], F32), "tdb": ("sbuf", [128, 32], F32), "tdc": ("sbuf", [128, 32], F32),
     "ic": ("sbuf", [128, 32], F32), "win": ("sbuf", [128, 16], BF), "win2": ("sbuf", [128, 16], BF),
-    "wme": ("sbuf", [128, 16], BF), "rst": ("sbuf", [128, C], BF), "rst7": ("sbuf", [128, 7 * 32], F32),
+    "wme": ("sbuf", [128, 16], BF), "rst": ("sbuf", [128, C], BF), "rst7": ("sbuf", [128, 7 * 32], BF),
     "cv": ("sbuf", [128, 128], F32), "cvb": ("sbuf", [128, 128], BF),
     "ji": ("sbuf", [128, 34], F32), "jm": ("sbuf", [128, 34], I32), "jf": ("sbuf", [128, 34], F32),
     "ja": ("sbuf", [128, 34], F32), "jb": ("sbuf", [128, 34], F32), "jc": ("sbuf", [128, 34], F32),
-    "sig": ("sbuf", [128, 34], U16), "dup": ("sbuf", [128, 32], U16), "pos": ("sbuf", [128, 32], F32),
-    "qc": ("sbuf", [128, 8], F32), "ba": ("sbuf", [128, 8], F32), "zr": ("sbuf", [128, 8], F32),
-    "mg": ("sbuf", [128, 8], F32),
+    "sig": ("sbuf", [128, 34], U16), "dup": ("sbuf", [128, 32], U16),
+    "pa": ("sbuf", [128, 4], F32), "pos": ("sbuf", [128, 32], F32),
+    "qc": ("sbuf", [128, 8], F32), "mg": ("sbuf", [128, 8], F32), "hm": ("sbuf", [128, 64], F32),
     "tw": ("sbuf", [128, 16], I32), "td16": ("sbuf", [128, 16], U16),
     "mk": ("sbuf", [128, C], BF), "jk": ("sbuf", [128, C], BF), "jn": ("sbuf", [128, C], F32),
     "dm": ("sbuf", [128, C], BF), "cc": ("sbuf", [128, C], BF),
     "xx": ("sbuf", [128, C], BF), "xc": ("sbuf", [128, C], BF),
     "s16": ("sbuf", [128, 8], U16), "inv": ("sbuf", [128, 272], BF), "gg": ("sbuf", [128, 544], BF),
     "yy": ("sbuf", [128, 544], BF), "lf": ("sbuf", [128, 18], F32), "lst1": ("sbuf", [128, 18], U16),
-    "cb": ("sbuf", [128, 4 * N], F32), "c7": ("sbuf", [128, 8], F32),
-    "zz": ("sbuf", [128, 48], F32),
-    "qa": ("sbuf", [128, 8], F32), "qi": ("sbuf", [128, 8], I32),
-    "aa": ("sbuf", [128, 8], F32), "jj": ("sbuf", [128, 8], F32),
-    "gr": ("sbuf", [128, 7 * 32], F32), "gs": ("sbuf", [128, 7 * 32], F32),
-    "l2t": ("sbuf", [128, 32], F32), "lst2": ("sbuf", [128, 22], U16),
+    "bn": ("sbuf", [128, 2], F32), "co": ("sbuf", [128, 4 * N], F32), "cb": ("sbuf", [128, 4 * N], F32),
+    "zz": ("sbuf", [128, 40], F32),
+    "jj": ("sbuf", [128, 8], F32), "gr": ("sbuf", [128, 7 * 32], BF), "gs": ("sbuf", [128, 7 * 32], BF),
+    "l2t": ("sbuf", [128, 32], BF), "lst2": ("sbuf", [128, 22], U16),
     "rd": ("dram", [128, 2], I32), "lr": ("dram", [N, 128, 2], I32),
     "tr": ("sbuf", [128, 16], I32), "tr16": ("sbuf", [128, 16], U16),
     "trd16": ("sbuf", [128, 16], U16), "mk3": ("sbuf", [128, C], BF), "kv": ("sbuf", [128, C], BF),
-    "vw": ("sbuf", [128, N * C], BF), "vl": ("sbuf", [128, C], BF),
-    "f1": ("sbuf", [128, 8], F32), "f2": ("sbuf", [128, 8], F32),
+    "vw": ("sbuf", [128, N * C], BF), "vl": ("sbuf", [128, C], BF), "f2": ("sbuf", [128, 8], F32),
     "ft": ("sbuf", [128, 32], F32), "w3": ("sbuf", [128, 512], F32), "y3": ("sbuf", [128, 512], F32),
-    "fa": ("sbuf", [128, 64], F32), "fb": ("sbuf", [128, 32], F32), "pk": ("sbuf", [128, 16], I32),
-    "ql": ("sbuf", [128, 16], I32), "qh": ("sbuf", [128, 16], I32), "qq": ("sbuf", [128, 16], I32),
-    "ua": ("sbuf", [128, 16], F32), "ub": ("sbuf", [128, 16], F32),
-    "uc": ("sbuf", [128, 16], F32), "ud": ("sbuf", [128, 16], F32), "lst3": ("sbuf", [128, 16], U16),
+    "fo": ("sbuf", [128, 128], F32), "hz": ("sbuf", [128, 64], F32), "ho": ("sbuf", [128, 64], F32),
+    "lst3": ("sbuf", [128, 16], U16),
     "xt": ("sbuf", [128, 4 * C], BF), "wt": ("sbuf", [128, 512], BF),
     "xq": ("sbuf", [128, C], CODES), "xs": ("sbuf", [128, C], PLANE),
     "wq": ("sbuf", [128, 128], CODES), "ws": ("sbuf", [128, 128], PLANE),
-    "out1q": ("sbuf", [128, 240], CODES), "out1s": ("sbuf", [128, 240], PLANE),
+    "out1q": ("sbuf", [128, 224], CODES), "out1s": ("sbuf", [128, 224], PLANE),
     "land1q": ("sbuf", [128, L1W], CODES), "land1s": ("sbuf", [128, L1W], PLANE),
     "out2q": ("sbuf", [128, 6 * S2], CODES), "out2s": ("sbuf", [128, 6 * S2], PLANE),
     "land2q": ("sbuf", [128, 7 * S2], CODES), "land2s": ("sbuf", [128, 7 * S2], PLANE),
     "fq": ("sbuf", [128, C], CODES), "fs": ("sbuf", [128, C], PLANE),
     "ps": ("psum", [128, 1024], F32), "ys": ("sbuf", [128, C], F32),
+    "via0": ("sbuf", [128, 4], F32),
+    "via1q": ("sbuf", [128, P1], CODES), "via1s": ("sbuf", [128, 3 * P1], PLANE),
+    "via2q": ("sbuf", [128, P2], CODES), "via2s": ("sbuf", [128, 2 * S2 + P2], PLANE),
 }
 SEMAPHORES = ["ev", "es", "eg", "et",
               "d_rd", "d_tw", "d_x", "d_w", "d_own", "d_tr", "d_vl", "d_y0", "d_y1",
               "a_raw", "a_cnt", "a_c1", "a_s1", "a_c2", "a_s2",
-              "l_raw", "l_cnt", "l_c1", "l_s1", "l_c2", "l_s2"]
+              "v_cnt", "v_1", "v_2",
+              "sent"]
+
+
+def land1_at(x):
+    return OWN1 if x == N - 1 else OWN1 + 48 + P1 * (2 - x) if x < 3 else 1 + P1 * (5 - x)
+
+
+def ways(T, topo, r):
+    core = T.cores[r]
+    peers = [T.cores[(r + 1 + x) % N] for x in range(N - 1)]
+    free = sorted((c for c in topo.cores_of(core) if c != core), key=lambda c: topo.die(c) == topo.die(core))
+    scales = [c for c in free if all(topo.may_write(c, p) for p in peers)][:2]
+    rest = [c for c in free if c not in scales]
+    codes = {}
+    for x, p in enumerate(peers):
+        if len(codes) < 2 and topo.may_write(rest[len(codes)], p):
+            codes[x] = rest[len(codes)]
+    return peers, scales, codes, [x for x in range(N - 1) if x not in codes]
 
 
 def rank_program(g, core, T, topo):
-    me = T.rank_of(core)
-    if me is None:
+    host = [T.rank_of(c) for c in topo.cores_of(core) if T.rank_of(c) is not None]
+    if not host:
         return
+    me = host[0]
+    peers, via_s, via_q, direct = ways(T, topo, me)
+    eng = [e for e in topo.engines(core, peers[0]) if all(e in topo.engines(core, p) for p in peers)]
+    u32, u8 = dt.uint32, dt.uint8
+    sent = [0]
+
+    def send(*transfers):
+        def dst(p):
+            rid, pid, _ = topo.addr(p)
+            return DstId(rid=rid, pnc=pid)
+        g.remote_dma_fused([RemoteDMATransfer(dst_ids=[dst(p) for p in to], dma_engine_mask=sum(1 << e for e in es),
+                                              remote_sem=T.sem[sem], srcs=[s], dsts=[d] * len(to))
+                            for s, d, to, es, sem in transfers], local_sem=T.sem.sent)
+        sent[0] += sum(len(t[3]) for t in transfers)
+
+    def deal(es, k):
+        return [es[i * len(es) // k:(i + 1) * len(es) // k] for i in range(k)]
+
+    hops = [(P1, P1, [land1_at(x) for x in range(N - 1)], "1"),
+            (S2, P2, [S2 * (N - 2 - x) for x in range(N - 1)], "2")]
+    mine = T.cb[:, 4 * me:4 * me + 4]
+
+    if core != T.cores[me]:
+        if core not in via_s and core not in via_q.values():
+            return
+        fed = len(topo.engines(T.cores[me], core))
+        g.wait_ge(T.sem.v_cnt, fed // 4)
+        if core in via_s:
+            i = via_s.index(core)
+            send((T.via0[:], mine, [peers[direct[i]]], eng, "a_cnt"))
+            for st, w, lnd, h in hops:
+                g.wait_ge(T.sem["v_" + h], fed // 2)
+                blocks = [(T["via%ss" % h][:, st * j:st * j + w], T["land%ss" % h][:, lnd[x]:lnd[x] + w], [peers[x]])
+                          for j, x in enumerate(range(3 * i, 3 * i + 3))]
+                send(*[b + (es, "a_s" + h) for b, es in zip(blocks[:2], deal(eng, 2))])
+                send(blocks[2] + (eng, "a_s" + h))
+        else:
+            x = [x for x in via_q if via_q[x] == core][0]
+            send((T.via0[:], mine, [peers[x]], eng, "a_cnt"))
+            for st, w, lnd, h in hops:
+                g.wait_ge(T.sem["v_" + h], fed // 2)
+                send((T["via%sq" % h][:].bitcast(u8), T["land%sq" % h][:, lnd[x]:lnd[x] + w].bitcast(u8), [peers[x]], eng,
+                      "a_c" + h))
+        g.wait_ge(T.sem.sent, sent[0])
+        return
+
     A, AF = AluOpType, ActivationFunctionType
     queue = {"v": g.vector, "s": g.scalar, "g": g, "t": g.tensor, "y": g.sync}
     count = {}
@@ -87,30 +151,23 @@ def rank_program(g, core, T, topo):
         return (sem, count[sem])
 
     V, S = g.vector, g.scalar
+    near = topo.engines(core, via_s[0])
+    slots = [((me - r - 1) % N, ways(T, topo, r)[3]) for r in range(N) if r != me]
+    got_q = sum(len(eng) // 4 if x in own else len(eng) for x, own in slots)
+    got_n = sum(len(eng) // 2 if x in own[2:] else len(eng) for x, own in slots)
+    got_s = 2 * 2 * len(eng)
 
-    peers = [T.cores[(me + 1 + x) % N] for x in range(N - 1)]
-    eng = [e for e in topo.engines(core, peers[0]) if all(e in topo.engines(core, p) for p in peers)]
-    ev, od = eng[0::2], eng[1::2]
-
-    def mask(es):
-        return sum(1 << e for e in es)
-
-    one = [[e] for e in ev] + [od[0:2], od[2:4]]
-    two = [ev[0:2], ev[2:4]] + [[e] for e in od]
-
-    def dst(p):
-        rid, pid, _ = topo.addr(p)
-        return DstId(rid=rid, pnc=pid)
-
-    def to_all(src, d, es, remote, local):
-        g.remote_dma_fused([RemoteDMATransfer(dst_ids=[dst(p) for p in peers], dma_engine_mask=mask(es),
-                                              remote_sem=T.sem[remote], srcs=[src], dsts=[d] * len(peers))],
-                           local_sem=T.sem[local])
-
-    def to_each(srcs, dsts, masks, remote, local):
-        g.remote_dma_fused([RemoteDMATransfer(dst_ids=[dst(p)], dma_engine_mask=mask(m), remote_sem=T.sem[remote],
-                                              src=s, dst=d) for p, s, d, m in zip(peers, srcs, dsts, masks)],
-                           local_sem=T.sem[local])
+    def hop(i, first, codes, scales):
+        st, w, lnd, h = hops[i]
+        oq, os_ = T["out%sq" % h], T["out%ss" % h]
+        wait("g", *scales)
+        send(*[(os_[:, first + 3 * st * j:first + 3 * st * j + 2 * st + w], T["via%ss" % h][:], [c], es, "v_" + h)
+               for j, (c, es) in enumerate(zip(via_s, deal(near, 2)))])
+        wait("g", *codes)
+        blk = [oq[:, first + st * x:first + st * x + w].bitcast(u8) for x in range(N - 1)]
+        send(*[(blk[x], T["via%sq" % h][:].bitcast(u8), [via_q[x]], es, "v_" + h) for x, es in zip(via_q, deal(near, 2))])
+        send(*[(blk[x], T["land%sq" % h][:, lnd[x]:lnd[x] + w].bitcast(u8), [peers[x]], es, "a_c" + h)
+               for x, es in zip(direct, deal(eng, 4))])
 
     rd = dma("y", "d_rd", T.rd[:], T.to[:])
     for i in range(8):
@@ -123,30 +180,40 @@ def rank_program(g, core, T, topo):
     k_ta = op("g", lambda: g.iota(T.ta[:], [[1, 11], [0, 3]], 0, 0, **flag))
     k_ic = op("g", lambda: g.iota(T.ic[:], [[0, 2], [1, 16]], 0, 0, **flag))
     k_ji = op("g", lambda: g.iota(T.ji[:], [[16, 17], [0, 2]], 0, 0, **flag))
-    k_tb = op("g", lambda: g.iota(T.tb[:, 0:32], [[16, 2], [0, 16]], 0, 0, **flag))
+    k_tb = op("g", lambda: g.iota(T.tb[:], [[16, 2], [0, 16]], 0, 0, **flag))
     k_cv = op("g", lambda: g.iota(T.cv[:], [[32, 8], [1, 16]], 0, 0, **flag))
     wait("g", rd)
     raw = eng[:1]
-    to_all(T.rd[:], T.lr[me], raw, "a_raw", "l_raw")
-    k_tc = op("g", lambda: g.iota(T.tb[:, 32:65], [[0, 11], [16, 3]], 0, 0, **flag))
+    send((T.rd[:], T.lr[me], peers, raw, "a_raw"))
 
     op("v", lambda: V.memset(T.dm[:, 0:1], -255.0))
     k_rst = op("v", lambda: V.memset(T.rst[:], 1.0))
     k_inv = op("v", lambda: V.memset(T.inv[:], 0.0))
     k_td3 = op("v", lambda: V.transpose(T.td3[:], T.ta[:, 0:32]), k_ta)
     k_mem = op("v", lambda: V.memset(T.rst[:, 0:C:32], 0.0), k_rst)
-    pd, p15, odd, pr = T.td3[:, 0:1], T.tdc[:, 0:1], T.tdb[:, 0:1], T.tdb[:, 32:33]
+    pd, p15, odd = T.td3[:, 0:1], T.tdc[:, 0:1], T.tdb[:, 0:1]
     k_win2 = op("v", lambda: V.tensor_scalar(T.win2[:], T.ic[:, 0:16], pd, None, A.is_lt), k_td3, k_ic)
     k_win = op("v", lambda: V.tensor_scalar(T.win[:], T.ic[:, 0:16], pd, 256.0, A.is_equal, A.mult))
     k_tdc = op("v", lambda: V.transpose(T.tdc[:], T.ic[:]))
     k_wme = op("v", lambda: V.tensor_scalar(T.wme[:], T.ic[:, 0:16], float(me), None, A.is_equal))
-    k_tdb = op("v", lambda: V.transpose(T.tdb[:, 0:32], T.tb[:, 0:32]), k_tb)
+    k_tdb = op("v", lambda: V.transpose(T.tdb[:], T.tb[:]), k_tb)
+
+    def fill(out, value):
+        n = out.shape[1]
+        src = T.ic[:, 0:n] if n <= 32 else T.rst[:, 0:n]
+        return op("s", lambda: S.activation(out, src, AF.Identity, bias=float(value), scale=0.0), k_ic, k_mem)
+
     k_jf = op("s", lambda: S.activation(T.jf[:], T.ji[:], AF.Identity, bias=p15), k_tdc, k_ji)
-    k_jm = op("v", lambda: V.tensor_scalar(T.jm[:], T.jf[:], -18.0, 1.0 / P1, A.add, A.mult), k_jf)
-    k_ja = op("s", lambda: S.activation(T.ja[:], T.jf[:], AF.Identity, bias=1.0, scale=7.0), k_jf)
+    k_jm = op("v", lambda: V.tensor_scalar(T.jm[:], T.jf[:], -20.0, 1.0 / P1, A.add, A.mult), k_jf)
+    k_ja = op("s", lambda: S.activation(T.ja[:], T.jf[:], AF.Identity, bias=-13.0, scale=7.0), k_jf)
+    k_dup = op("v", lambda: V.tensor_copy(T.dup[:], T.jf[:, 0:32]))
+    for a, b in ((0, 3), (3, 6), (6, 7)):
+        k_qc = op("s", lambda: S.activation(T.qc[:, a:b], T.ic[:, a:b], AF.Identity, scale=-1.0 - 7 * P1,
+                                            bias=3.0 + 7 * (land1_at(a) + P1 * a)))
+    k_mg = fill(T.mg[:], -R23)
 
     k_td = op("v", lambda: V.tensor_scalar(T.td16[:], T.tw[:], -127.5, 1.0 / C, A.add, A.mult), tw)
-    bm, nm = T.cb[:, 4 * me:4 * me + 1], T.cb[:, 4 * me + 1:4 * me + 2]
+    bm, nm = T.bn[:, 0:1], T.bn[:, 1:2]
     k_b = op("s", lambda: S.activation(T.jk[:], T.win2[:].indirect(T.td16[:]), AF.Identity, accum_out=bm), k_td, k_win2)
     k_jb = op("v", lambda: V.tensor_scalar(T.jb[:], T.jm[:], float(1 - 7 * P1), None, A.mult), k_jm)
     k_mk = op("v", lambda: V.tensor_copy(T.mk[:], T.win[:].indirect(T.td16[:])), k_td, k_win)
@@ -159,147 +226,125 @@ def rank_program(g, core, T, topo):
     k_xx = op("v", lambda: V.transpose(T.xx[:], T.cc[:]), k_cc)
     k_xc = op("v", lambda: V.tensor_tensor_scan(T.xc[:], T.rst[:], T.xx[:], 0.0, A.mult, A.max), k_xx, k_mem)
     k_s = op("v", lambda: V.tensor_copy(T.s16[:], T.xc[:, 31:C:32]), k_xc)
+    c_v, c_w, c_7, c_u = (T.co[:, i:4 * N:4] for i in range(4))
+    k_u = op("s", lambda: S.activation(c_u, T.qc[:, 0:N], AF.Identity, bias=bm), k_b, k_qc)
+    k_c7 = op("s", lambda: S.activation(c_7, T.mg[:, 0:N], AF.Identity, bias=nm, scale=-1.0), k_nm, k_mg)
+    op("s", lambda: S.activation(c_v, c_u, AF.Identity, bias=R23, scale=1.0 / 7), k_u)
+    k_co = op("s", lambda: S.activation(c_w, c_u, AF.Identity, bias=T.co[:, 2:3], scale=1.0 / 7), k_c7)
     k_cvb = op("s", lambda: S.activation(T.cvb[:], T.cv[:], AF.Identity, bias=odd), k_cv, k_tdb)
     k_sc = op("v", lambda: V.tensor_copy(T.inv[:].indirect(T.s16[:]), T.cvb[:]), k_s, k_cvb, k_inv)
-
-    def lin(out, a, b, scale, bias):
-        return op("s", lambda: S.activation(out[:, a:b], T.ic[:, a:b], AF.Identity, bias=float(bias), scale=float(scale)),
-                  k_ic)
-
-    fp, rx, aj = T.zz[:, 0:32], 32, 40
-    k_zz = op("s", lambda: S.activation(T.zz[:], T.cv[:, 0:48], AF.Copy, scale=0.0))
-    k_mg = lin(T.mg, 0, 8, 0, -R23)
-    op("s", lambda: S.activation(T.rst7[:, 0:128], T.cv[:], AF.Identity, bias=1.0, scale=0.0))
-    k_r7 = op("s", lambda: S.activation(T.rst7[:, 128:224], T.cv[:, 0:96], AF.Identity, bias=1.0, scale=0.0))
-    k_r7 = op("s", lambda: S.activation(T.rst7[:, 0:224:7], T.cv[:, 0:32], AF.Copy, scale=0.0), k_r7)
+    k_vw = fill(T.vw[:, C * me:C * me + C], -4096)
 
     k_ga = op("s", lambda: S.activation(T.gg[:, 0:CA], T.inv[:].indirect(T.sig[:, 0:CA // 16]), AF.Copy), k_sc, k_sig)
-    k_gb = op("v", lambda: V.tensor_copy(T.gg[:, CA:544], T.inv[:].indirect(T.sig[:, CA // 16:34])), k_sc, k_sig)
+    k_gb = op("v", lambda: V.tensor_copy(T.gg[:, CA:448], T.inv[:].indirect(T.sig[:, CA // 16:28])), k_sc, k_sig)
     k_xq = op("v", lambda: V.quantize_mx(T.xq[:], T.xs[:], T.xt[:]), xl)
-    k_yy = op("v", lambda: V.transpose(T.yy[:], T.gg[:]), k_ga, k_gb)
-    k_lf = op("v", lambda: V.tensor_tensor(T.lf[:, 0:17], T.yy[:, 0:544:32], T.yy[:, 16:544:32], A.add), k_yy)
-    k_l1 = op("v", lambda: V.tensor_copy(T.lst1[:, 0:17], T.lf[:, 0:17]), k_lf)
-    k_qc = lin(T.qc, 0, me + 1, 1, 3 - me)
-    if me < N - 1:
-        k_qc = lin(T.qc, me + 1, N, 1, 3 - me - N)
+    k_yy = op("v", lambda: V.transpose(T.yy[:, 0:448], T.gg[:, 0:448]), k_ga, k_gb)
+    k_gc = op("s", lambda: S.activation(T.gg[:, 448:544], T.inv[:].indirect(T.sig[:, 28:34]), AF.Copy))
+    k_lf = op("v", lambda: V.tensor_tensor(T.lf[:, 0:14], T.yy[:, 0:448:32], T.yy[:, 16:448:32], A.add), k_yy)
+    k_yz = op("v", lambda: V.transpose(T.yy[:, 448:544], T.gg[:, 448:544]), k_gc)
+    k_l1 = op("v", lambda: V.tensor_copy(T.lst1[:, 0:14], T.lf[:, 0:14]), k_lf)
+    k_lg = op("v", lambda: V.tensor_tensor(T.lf[:, 14:17], T.yy[:, 448:544:32], T.yy[:, 464:544:32], A.add), k_yz)
 
-    wait("g", k_nm)
-    to_all(T.cb[:, 4 * me:4 * me + 2], T.cb[:, 4 * me:4 * me + 2], eng, "a_cnt", "l_cnt")
+    wait("g", k_co)
+    told = [T.co[:, 4 * x:4 * x + 4] for x in range(N)]
+    send(*[(told[x], T.via0[:], [c], es, "v_cnt")
+           for x, c, es in zip(direct[:2] + list(via_q), via_s + list(via_q.values()), deal(near, 4))])
+    send(*[(told[x], mine, [peers[x]], es, "a_cnt") for x, es in zip(direct[2:], deal(eng, 2))])
 
-    lo, la = T.lst1[:, 2:17], T.lst1[:, 0:3]
-    u32, u8 = dt.uint32, dt.uint8
-    k_p1 = op("v", lambda: V.tensor_copy(T.out1q[:].bitcast(u32), T.xq[:].bitcast(u32).indirect(lo)), k_l1, k_xq)
-    k_o1 = op("s", lambda: S.activation(T.out1s[:], T.xs[:].indirect(lo), AF.Copy), k_l1, k_xq)
-    wait("g", k_p1)
-    blk = [P1 * (x + 1) - 32 for x in range(N - 1)]
-    lnd = [48 + P1 * x for x in range(N - 1)]
-    to_each([T.out1q[:, a:a + P1].bitcast(u8) for a in blk], [T.land1q[:, a:a + P1].bitcast(u8) for a in lnd], one,
-            "a_c1", "l_c1")
-    wait("g", k_o1)
-    to_each([T.out1s[:, a:a + P1] for a in blk], [T.land1s[:, a:a + P1] for a in lnd], two, "a_s1", "l_s1")
-    k_a1 = op("v", lambda: V.tensor_copy(T.land1q[:, 0:48].bitcast(u32), T.xq[:].bitcast(u32).indirect(la)))
-    k_tdd = op("v", lambda: V.transpose(T.tdb[:, 32:64], T.tb[:, 32:64]), k_tc)
-    k_b1 = op("s", lambda: S.activation(T.land1s[:, 0:48], T.xs[:].indirect(la), AF.Copy))
+    def pick(lst, a, b, oq, os_, q, s, for_q, for_s):
+        parts = [(slice(0, 16 * a), lst[:, 0:a]), (slice(16 * a, 16 * b), lst[:, a:b])]
+        ks = [op("s", lambda: S.activation(os_[:, parts[0][0]], s[:].indirect(parts[0][1]), AF.Copy), *for_s),
+              op("v", lambda: V.tensor_copy(os_[:, parts[1][0]], s[:].indirect(parts[1][1])), *for_s)]
+        kq = [op("v", lambda: V.tensor_copy(oq[:, c].bitcast(u32), q[:].bitcast(u32).indirect(o)), *for_q)
+              for c, o in parts]
+        return kq, ks
 
+    la = T.lst1[:, 14:17]
+    hop(0, 2, *pick(T.lst1, 8, 14, T.out1q, T.out1s, T.xq, T.xs, [], [k_l1, k_xq]))
     k_vl = op("g", lambda: g.iota(T.vl[:], [[0, C]], 0, 0, **flag))
 
     dma("y", "d_tr", T.tr[112:128, :], T.to[:])
     tr = dma("y", "d_tr", T.tr[0:112, :], T.lr[:], own, ("a_raw", 6 * len(raw)))
 
-    k_pos = op("s", lambda: S.activation(T.pos[:], T.ic[:], AF.Identity, bias=pr), k_tdd)
-    if me < N - 1:
-        lin(T.ba, me + 1, N, -P1, 48 - P1 + P1 * (me + N))
-    if me > 0:
-        lin(T.ba, 0, me, -P1, 48 - P1 + P1 * me)
-    k_ba = lin(T.ba, me, me + 1, 0, 0)
-    k_vw = op("s", lambda: S.activation(T.vw[:, C * me:C * me + C], T.rst[:], AF.Identity, bias=-4096.0, scale=0.0),
-              k_mem)
-
-    bb, nn = T.cb[:, 0:4 * N:4], T.cb[:, 1:4 * N:4]
-    cn = ("a_cnt", 6 * len(eng))
-    k_c7 = op("v", lambda: V.tensor_scalar(T.c7[:, 0:N], nn, R23, None, A.add), cn, k_nm)
-    k_q = op("v", lambda: V.tensor_tensor(T.qa[:, 0:N], bb, T.qc[:, 0:N], A.add), k_qc, k_b)
-    k_rx = op("v", lambda: V.tensor_tensor_scan(T.zz[:, rx + 1:rx + 8], T.c7[:, 0:N], T.mg[:, 0:N], 0.0, A.add, A.add),
-              k_c7, k_mg, k_zz)
-    k_qi = op("v", lambda: V.tensor_scalar(T.qi[:, 0:N], T.qa[:, 0:N], 1.0 / 7, None, A.mult), k_q)
-    k_aa = op("v", lambda: V.tensor_tensor(T.aa[:, 0:N], T.qi[:, 0:N], T.ba[:, 0:N], A.add), k_qi, k_ba)
-    kb = op("v", lambda: V.tensor_copy(T.tr16[:], T.tr[:]), tr)
-    k_a = op("v", lambda: V.tensor_tensor(T.zz[:, aj + 1:aj + 8], T.aa[:, 0:N], T.zz[:, rx:rx + N], A.subtract),
-             k_rx, k_aa)
-    k_t3 = op("v", lambda: V.tensor_scalar(T.trd16[:], T.tr[:], -127.5, 1.0 / C, A.add, A.mult))
-    k_jj = op("v", lambda: V.tensor_tensor(T.jj[:, 0:N], T.zz[:, aj + 1:aj + 8], T.zz[:, aj:aj + N], A.subtract), k_a)
+    k_lo = op("v", lambda: V.tensor_copy(la, T.lf[:, 14:17]), k_lg)
+    k_t3 = op("v", lambda: V.tensor_scalar(T.trd16[:], T.tr[:], -127.5, 1.0 / C, A.add, A.mult), tr)
+    kb = op("v", lambda: V.tensor_copy(T.tr16[:], T.tr[:]))
     k_mk3 = op("s", lambda: S.activation(T.mk3[:], T.wme[:].indirect(T.trd16[:]), AF.Copy), k_t3, k_wme)
-    k_zr = lin(T.zr, 0, N, 1, 12 - me)
-    k_gr = op("v", lambda: V.tensor_scalar(T.gr[:, 0:224:7], T.pos[:], T.jj[:, 0:1], None, A.add), k_jj, k_pos)
-    for r in range(1, N):
-        k_gr = op("v", lambda: V.tensor_scalar(T.gr[:, r:224:7], T.pos[:], T.zz[:, rx + r:rx + r + 1], T.jj[:, r:r + 1],
-                                               A.is_ge, A.mult))
-    k = op("v", lambda: V.tensor_tensor_scan(T.gs[:], T.rst7[:], T.gr[:], 0.0, A.mult, A.add), k_gr, k_r7)
-    k = op("v", lambda: V.transpose(T.l2t[:], T.gs[:, 6:224:7]), k)
-    e = 3 * (N - 1 - me)
-    if e:
-        op("v", lambda: V.tensor_scalar(T.lst2[:, 0:e], T.l2t[:, 3 * (me + 1):21], float(L1W - 1), None, A.min), k)
-    k_l2 = op("v", lambda: V.tensor_scalar(T.lst2[:, e:21], T.l2t[:, 0:3 * (me + 1)], float(L1W - 1), None, A.min), k)
-
+    k_b1 = op("s", lambda: S.activation(T.land1s[:, OWN1:OWN1 + 48], T.xs[:].indirect(la), AF.Copy), k_lo)
+    k_a1 = op("v", lambda: V.tensor_copy(T.land1q[:, OWN1:OWN1 + 48].bitcast(u32), T.xq[:].bitcast(u32).indirect(la)),
+              k_lo)
+    k_wq = op("v", lambda: V.quantize_mx(T.wq[:], T.ws[:], T.wt[:]), wl)
     k = op("v", lambda: V.tensor_tensor_scan(T.kv[:], T.mk3[:], T.mk3[:], 0.0, A.add, A.max), k_mk3)
     k_v = op("v", lambda: V.tensor_copy(T.vw[:].indirect(T.tr16[:]), T.kv[:]), k, kb, k_vw)
     for i in range(4):
         vl = dma("y", "d_vl", T.vl[32 * i:32 * i + 4 * N:4, :], T.vw[0:16 * N:16, C * me:C * me + C], k_v, k_vl)
 
-    lo, la = T.lst2[:, 0:18], T.lst2[:, 18:21]
-    c1, s1 = ("a_c1", 8), ("a_s1", 8)
-    k_p2 = op("v", lambda: V.tensor_copy(T.out2q[:].bitcast(u32), T.land1q[:].bitcast(u32).indirect(lo)),
-              k_l2, k_a1, c1)
-    k_o2 = op("s", lambda: S.activation(T.out2s[:], T.land1s[:].indirect(lo), AF.Copy), k_l2, k_b1, s1)
-    wait("g", k_p2)
-    blk = [S2 * x for x in range(N - 1)]
-    lnd = [S2 * (N - 2 - x) for x in range(N - 1)]
-    to_each([T.out2q[:, a:a + P2].bitcast(u8) for a in blk], [T.land2q[:, a:a + P2].bitcast(u8) for a in lnd], one,
-            "a_c2", "l_c2")
-    wait("g", k_o2)
-    to_each([T.out2s[:, a:a + P2] for a in blk], [T.land2s[:, a:a + P2] for a in lnd], two, "a_s2", "l_s2")
+    fp, rx = T.zz[:, 0:32], 32
+    k_me = op("s", lambda: S.activation(mine, told[N - 1], AF.Copy), k_co)
+    k = op("s", lambda: S.activation(T.pa[:, 0:1], pd, AF.Identity, bias=p15, scale=-3.0))
+    k_zz = fill(T.zz[:], 0)
+    k = op("s", lambda: S.activation(T.pa[:, 1:2], T.pa[:, 0:1], AF.Identity, bias=odd), k)
+    k_r7 = fill(T.rst7[:], 1)
+    k = op("s", lambda: S.activation(T.pa[:, 2:3], T.pa[:, 1:2], AF.Identity, scale=16.0), k)
+    k_r7 = op("s", lambda: S.activation(T.rst7[:, 0:224:7], T.ic[:], AF.Copy, scale=0.0), k_r7)
+    k_pos = op("s", lambda: S.activation(T.pos[:], T.ic[:], AF.Identity, bias=T.pa[:, 2:3]), k)
+    fill(T.hz[:, 1:64:4], -R23)
+    for i, m in enumerate((0, 1, -7, S2)):
+        k_hm = fill(T.hm[:, i:64:4], m)
+
+    k_jj = op("v", lambda: V.tensor_tensor(T.jj[:, 1:N], T.cb[:, 4:4 * N:4], T.cb[:, 1:4 * N - 4:4], A.subtract),
+              ("a_cnt", got_n), k_me)
+    k_rx = op("v", lambda: V.tensor_tensor_scan(T.zz[:, rx + 1:rx + 8], T.cb[:, 2:4 * N:4], T.mg[:, 0:N], 0.0,
+                                                A.add, A.add), k_zz)
+    op("v", lambda: V.tensor_scalar(T.gr[:, 0:224:7], T.pos[:], T.cb[:, 0:1], -128.0 - R23, A.add, A.add), k_pos)
+    for r in range(1, N):
+        k_gr = op("v", lambda: V.tensor_scalar(T.gr[:, r:224:7], T.pos[:], T.zz[:, rx + r:rx + r + 1], T.jj[:, r:r + 1],
+                                               A.is_ge, A.mult), k_jj, k_rx)
+    k_f2 = op("v", lambda: V.tensor_scalar(T.f2[:, 0:N], T.zz[:, rx:rx + N], 7.0 * U, float(SHIFT - U), A.mult, A.add))
+    k = op("v", lambda: V.tensor_tensor_scan(T.gs[:], T.rst7[:], T.gr[:], 0.0, A.mult, A.add), k_gr, k_r7)
+    k_f = op("v", lambda: V.tensor_tensor(T.zz[:, 0:4 * N:4], T.cb[:, 3:4 * N:4], T.f2[:, 0:N], A.add), k_f2)
+    k = op("v", lambda: V.transpose(T.l2t[:], T.gs[:, 6:224:7]), k)
+    k_ft = op("v", lambda: V.transpose(T.ft[:], fp), k_f)
+    e = 3 * (N - 1 - me)
+    top = (128.0, float(L1W - 1), A.add, A.min)
+    if e:
+        op("v", lambda: V.tensor_scalar(T.lst2[:, 0:e], T.l2t[:, 3 * (me + 1):21], *top), k)
+    k_l2 = op("v", lambda: V.tensor_scalar(T.lst2[:, e:21], T.l2t[:, 0:3 * (me + 1)], *top), k)
+
+    la = T.lst2[:, 18:21]
+    hop(1, 0, *pick(T.lst2, 10, 18, T.out2q, T.out2s, T.land1q, T.land1s, [k_a1, ("a_c1", got_q)],
+                    [k_l2, k_b1, ("a_s1", got_s)]))
     k_a2 = op("v", lambda: V.tensor_copy(T.land2q[:, 6 * S2:7 * S2].bitcast(u32),
                                          T.land1q[:].bitcast(u32).indirect(la)))
-    k_f1 = op("v", lambda: V.tensor_tensor(T.f1[:, 0:N], bb, T.zr[:, 0:N], A.add), k_zr)
-    k_f2 = op("v", lambda: V.tensor_scalar(T.f2[:, 0:N], T.zz[:, rx:rx + N], 7.0 * U, -1.0 * U, A.mult, A.add))
-    k_f = op("v", lambda: V.tensor_tensor(T.zz[:, 0:4 * N:4], T.f1[:, 0:N], T.f2[:, 0:N], A.add), k_f2)
-    k_dup = op("v", lambda: V.tensor_copy(T.dup[:], T.jf[:, 0:32]))
-    k_ft = op("v", lambda: V.transpose(T.ft[:], fp), k_f)
-    k_wq = op("v", lambda: V.quantize_mx(T.wq[:], T.ws[:], T.wt[:]), wl)
 
-    for i in range(2):
-        h = slice(256 * i, 256 * i + 256)
-        k = op("s", lambda: S.activation(T.w3[:, h], T.vl[:].indirect(T.dup[:, 16 * i:16 * i + 16]), AF.Relu,
-                                         bias=T.ft[:, 3 * me:3 * me + 1], scale=float(U + 1)), vl, k_ft, k_dup)
-        k = op("v", lambda: V.transpose(T.y3[:, h], T.w3[:, h]), k)
+    kw = [op("s", lambda: S.activation(T.w3[:, 256 * i:256 * i + 256], T.vl[:].indirect(T.dup[:, 16 * i:16 * i + 16]),
+                                       AF.Relu, bias=T.ft[:, 3 * me:3 * me + 1], scale=float(U)), vl, k_ft, k_dup)
+          for i in range(2)]
     k_b2 = op("s", lambda: S.activation(T.land2s[:, 6 * S2:7 * S2], T.land1s[:].indirect(la), AF.Copy))
-    k = op("v", lambda: V.tensor_tensor(T.fa[:], T.y3[:, 0:512:8], T.y3[:, 4:512:8], A.add), k)
-    k = op("v", lambda: V.tensor_tensor(T.fb[:], T.fa[:, 0:64:2], T.fa[:, 1:64:2], A.add), k)
-    k = op("v", lambda: V.tensor_tensor(T.pk[:], T.fb[:, 0:32:2], T.fb[:, 1:32:2], A.add), k)
-    kl = op("v", lambda: V.tensor_scalar(T.ql[:], T.pk[:], U - 1, None, A.bitwise_and), k)
-    kh = op("v", lambda: V.tensor_scalar(T.qh[:], T.pk[:], 0.5 - 3.5 * U, 1.0 / (7 * U), A.add, A.mult))
-    kq = op("v", lambda: V.tensor_scalar(T.qq[:], T.ql[:], -3.0, 1.0 / 7, A.add, A.mult), kl)
-    ka = op("v", lambda: V.tensor_scalar(T.ua[:], T.ql[:], float(S2), None, A.mult))
-    kb = op("v", lambda: V.tensor_scalar(T.ub[:], T.qq[:], -7.0 * S2, None, A.mult), kq)
-    kc = op("v", lambda: V.tensor_tensor(T.uc[:], T.ua[:], T.qh[:], A.add), ka, kh)
-    kd = op("v", lambda: V.tensor_tensor(T.ud[:], T.ub[:], T.uc[:], A.add), kb, kc)
-    k_l3 = op("v", lambda: V.tensor_copy(T.lst3[:], T.ud[:]), kd)
+    for i in range(2):
+        k = op("v", lambda: V.transpose(T.y3[:, 256 * i:256 * i + 256], T.w3[:, 256 * i:256 * i + 256]), kw[i])
+        k = op("v", lambda: V.tensor_tensor_scan(T.fo[:, 64 * i:64 * i + 64], T.rst[:, 0:C:4],
+                                                 T.y3[:, 256 * i:256 * i + 256:4], 0.0, A.mult, A.add), k)
+    z = T.fo[:, 7:128:8]
+    op("v", lambda: V.tensor_scalar(T.hz[:, 0:64:4], z, 1.0 / 7, R23, A.mult, A.add), k)
+    op("v", lambda: V.tensor_copy(T.hz[:, 2:64:4], z))
+    k = op("v", lambda: V.tensor_scalar(T.hz[:, 3:64:4], z, 1.0 / (7 * U), R23, A.mult, A.add))
+    k = op("v", lambda: V.tensor_tensor_scan(T.ho[:], T.hm[:], T.hz[:], 0.0, A.mult, A.add), k, k_hm)
+    k_l3 = op("v", lambda: V.tensor_scalar(T.lst3[:], T.ho[:, 3:64:4], 3.0 * S2 - 1 - R23, None, A.add), k)
 
-    c2, s2 = ("a_c2", 8), ("a_s2", 8)
+    c2, s2 = ("a_c2", got_q), ("a_s2", got_s)
     cols = [slice(128 * i, 128 * i + 128) for i in range(2)]
     lst = [T.lst3[:, 8 * i:8 * i + 8] for i in range(2)]
     kq = [op("v", lambda: V.tensor_copy(T.fq[:, cols[i]].bitcast(u32), T.land2q[:].bitcast(u32).indirect(lst[i])),
              k_l3, k_a2, c2) for i in range(2)]
-    ks = [op("s", lambda: S.activation(T.fs[:, cols[0]], T.land2s[:].indirect(lst[0]), AF.Copy), k_l3, k_b2, s2),
-          op("v", lambda: V.tensor_copy(T.fs[:, cols[1]], T.land2s[:].indirect(lst[1])), k_b2, s2)]
+    ks = [op("s", lambda: S.activation(T.fs[:, cols[i]], T.land2s[:].indirect(lst[i]), AF.Copy), k_l3, k_b2, s2)
+          for i in range(2)]
     mm = [op("t", lambda: g.tensor.matmul_mx(T.ps[:, 512 * i:512 * i + 128], T.wq[:], T.ws[:], T.fq[:, cols[i]],
                                              T.fs[:, cols[i]], True, True), kq[i], ks[i], k_wq) for i in range(2)]
-    k0 = op("s", lambda: S.activation(T.ys[:, 0:128], T.ps[:, 0:128], AF.Copy), mm[0])
-    k1 = op("v", lambda: V.tensor_copy(T.ys[:, 128:256], T.ps[:, 512:640]), mm[1])
-    y0 = dma("s", "d_y0", T.y[:, 0:128], T.ys[:, 0:128], k0)
-    y1 = dma("y", "d_y1", T.y[:, 128:256], T.ys[:, 128:256], k1)
+    k0 = op("v", lambda: V.tensor_copy(T.ys[:, 0:128], T.ps[:, 0:128]), mm[0])
+    k1 = op("s", lambda: S.activation(T.ys[:, 128:256], T.ps[:, 512:640], AF.Copy), mm[1])
+    y0 = dma("y", "d_y0", T.y[:, 0:128], T.ys[:, 0:128], k0)
+    y1 = dma("s", "d_y1", T.y[:, 128:256], T.ys[:, 128:256], k1)
 
-    wait("g", ("l_raw", len(raw)))
-    for sem in ("l_cnt", "l_c1", "l_s1", "l_c2", "l_s2"):
-        wait("g", (sem, len(eng)))
+    wait("g", ("sent", sent[0]))
     wait("y", y0, y1, *[(s, count[s]) for s in ("ev", "es", "eg", "et")])

@@ -5,9 +5,11 @@ N, C = 7, 256
 P1, P2, S2 = 37, 42, 48
 OWN1 = 112
 L1W = OWN1 + 48 + 3 * P1
+L2 = 4
+L2W = L2 + 6 * P2 + 48
 U = 4096
 SHIFT = 7 * U - 13300
-CA = 288
+CA = 256
 R23 = 12582912.0
 
 F32, BF, I32, U16, CODES, PLANE = "float32", "bfloat16", "int32", "uint16", "float8_e4m3fn_x4", "uint8"
@@ -17,18 +19,18 @@ SCRATCH = {
     "ic": ("sbuf", [128, 32], F32), "win": ("sbuf", [128, 16], BF), "win2": ("sbuf", [128, 16], BF),
     "wme": ("sbuf", [128, 16], BF), "rst": ("sbuf", [128, C], BF), "rst7": ("sbuf", [128, 7 * 32], BF),
     "cv": ("sbuf", [128, 128], F32), "cvb": ("sbuf", [128, 128], BF),
-    "ji": ("sbuf", [128, 34], F32), "jm": ("sbuf", [128, 34], I32), "jf": ("sbuf", [128, 34], F32),
+    "ji": ("sbuf", [128, 34], F32), "jm": ("sbuf", [128, 34], F32), "jf": ("sbuf", [128, 34], F32),
     "ja": ("sbuf", [128, 34], F32), "jb": ("sbuf", [128, 34], F32), "jc": ("sbuf", [128, 34], F32),
     "sig": ("sbuf", [128, 34], U16), "dup": ("sbuf", [128, 32], U16),
-    "pa": ("sbuf", [128, 4], F32), "pos": ("sbuf", [128, 32], F32),
-    "qc": ("sbuf", [128, 8], F32), "mg": ("sbuf", [128, 8], F32), "hm": ("sbuf", [128, 64], F32),
+    "pa": ("sbuf", [128, 4], F32), "pos": ("sbuf", [128, 32], F32), "low": ("sbuf", [128, 32], F32),
+    "qc": ("sbuf", [128, 8], F32), "hm": ("sbuf", [128, 64], F32),
     "tw": ("sbuf", [128, 16], I32), "td16": ("sbuf", [128, 16], U16),
     "mk": ("sbuf", [128, C], BF), "jk": ("sbuf", [128, C], BF), "jn": ("sbuf", [128, C], F32),
     "dm": ("sbuf", [128, C], BF), "cc": ("sbuf", [128, C], BF),
     "xx": ("sbuf", [128, C], BF), "xc": ("sbuf", [128, C], BF),
     "s16": ("sbuf", [128, 8], U16), "inv": ("sbuf", [128, 272], BF), "gg": ("sbuf", [128, 544], BF),
     "yy": ("sbuf", [128, 544], BF), "lf": ("sbuf", [128, 18], F32), "lst1": ("sbuf", [128, 18], U16),
-    "bn": ("sbuf", [128, 2], F32), "co": ("sbuf", [128, 4 * N], F32), "cb": ("sbuf", [128, 4 * N], F32),
+    "bn": ("sbuf", [128, 4], F32), "co": ("sbuf", [128, 3 * N], F32), "cb": ("sbuf", [128, 4 * N], F32),
     "zz": ("sbuf", [128, 40], F32),
     "jj": ("sbuf", [128, 8], F32), "gr": ("sbuf", [128, 7 * 32], BF), "gs": ("sbuf", [128, 7 * 32], BF),
     "l2t": ("sbuf", [128, 32], BF), "lst2": ("sbuf", [128, 22], U16),
@@ -45,12 +47,12 @@ SCRATCH = {
     "out1q": ("sbuf", [128, 224], CODES), "out1s": ("sbuf", [128, 224], PLANE),
     "land1q": ("sbuf", [128, L1W], CODES), "land1s": ("sbuf", [128, L1W], PLANE),
     "out2q": ("sbuf", [128, 6 * S2], CODES), "out2s": ("sbuf", [128, 6 * S2], PLANE),
-    "land2q": ("sbuf", [128, 7 * S2], CODES), "land2s": ("sbuf", [128, 7 * S2], PLANE),
+    "land2q": ("sbuf", [128, L2W], CODES), "land2s": ("sbuf", [128, L2W], PLANE),
     "fq": ("sbuf", [128, C], CODES), "fs": ("sbuf", [128, C], PLANE),
     "ps": ("psum", [128, 1024], F32), "ys": ("sbuf", [128, C], F32),
-    "via0": ("sbuf", [128, 4], F32),
-    "via1q": ("sbuf", [128, P1], CODES), "via1s": ("sbuf", [128, 3 * P1], PLANE),
-    "via2q": ("sbuf", [128, P2], CODES), "via2s": ("sbuf", [128, 2 * S2 + P2], PLANE),
+    "via0": ("sbuf", [128, 6], F32),
+    "via1q": ("sbuf", [128, P1], CODES), "via1s": ("sbuf", [128, 2 * P1], PLANE),
+    "via2q": ("sbuf", [128, P2], CODES), "via2s": ("sbuf", [128, S2 + P2], PLANE),
 }
 SEMAPHORES = ["ev", "es", "eg", "et",
               "d_rd", "d_tw", "d_x", "d_w", "d_own", "d_tr", "d_vl", "d_y0", "d_y1",
@@ -67,8 +69,8 @@ def ways(T, topo, r):
     core = T.cores[r]
     peers = [T.cores[(r + 1 + x) % N] for x in range(N - 1)]
     free = sorted((c for c in topo.cores_of(core) if c != core), key=lambda c: topo.die(c) == topo.die(core))
-    scales = [c for c in free if all(topo.may_write(c, p) for p in peers)][:2]
-    rest = [c for c in free if c not in scales]
+    scales = [c for c in free if all(topo.may_write(c, p) for p in peers)][:3]
+    rest = [c for c in free if topo.die(c) == topo.die(core) and c not in scales]
     codes = {}
     for x, p in enumerate(peers):
         if len(codes) < 2 and topo.may_write(rest[len(codes)], p):
@@ -99,28 +101,28 @@ def rank_program(g, core, T, topo):
         return [es[i * len(es) // k:(i + 1) * len(es) // k] for i in range(k)]
 
     hops = [(P1, P1, [land1_at(x) for x in range(N - 1)], "1"),
-            (S2, P2, [S2 * (N - 2 - x) for x in range(N - 1)], "2")]
-    mine = T.cb[:, 4 * me:4 * me + 4]
+            (S2, P2, [L2 + P2 * (N - 2 - x) for x in range(N - 1)], "2")]
+    mine = T.cb[:, 4 * me:4 * me + 3]
 
     if core != T.cores[me]:
         if core not in via_s and core not in via_q.values():
             return
         fed = len(topo.engines(T.cores[me], core))
-        g.wait_ge(T.sem.v_cnt, fed // 4)
+        g.wait_ge(T.sem.v_cnt, fed if core == via_s[2] else fed // 4)
         if core in via_s:
             i = via_s.index(core)
-            send((T.via0[:], mine, [peers[direct[i]]], eng, "a_cnt"))
+            told = [direct[0:2], direct[2:3], direct[3:4]][i]
+            send(*[(T.via0[:, 3 * j:3 * j + 3], mine, [peers[x]], es, "a_cnt")
+                   for j, (x, es) in enumerate(zip(told, deal(eng, len(told))))])
             for st, w, lnd, h in hops:
-                g.wait_ge(T.sem["v_" + h], fed // 2)
-                blocks = [(T["via%ss" % h][:, st * j:st * j + w], T["land%ss" % h][:, lnd[x]:lnd[x] + w], [peers[x]])
-                          for j, x in enumerate(range(3 * i, 3 * i + 3))]
-                send(*[b + (es, "a_s" + h) for b, es in zip(blocks[:2], deal(eng, 2))])
-                send(blocks[2] + (eng, "a_s" + h))
+                g.wait_ge(T.sem["v_" + h], fed // 2 if i < 2 else fed)
+                send(*[(T["via%ss" % h][:, st * j:st * j + w], T["land%ss" % h][:, lnd[x]:lnd[x] + w], [peers[x]], es,
+                        "a_s" + h) for j, (x, es) in enumerate(zip((2 * i, 2 * i + 1), deal(eng, 2)))])
         else:
             x = [x for x in via_q if via_q[x] == core][0]
-            send((T.via0[:], mine, [peers[x]], eng, "a_cnt"))
+            send((T.via0[:, 0:3], mine, [peers[x]], eng, "a_cnt"))
             for st, w, lnd, h in hops:
-                g.wait_ge(T.sem["v_" + h], fed // 2)
+                g.wait_ge(T.sem["v_" + h], fed // 4)
                 send((T["via%sq" % h][:].bitcast(u8), T["land%sq" % h][:, lnd[x]:lnd[x] + w].bitcast(u8), [peers[x]], eng,
                       "a_c" + h))
         g.wait_ge(T.sem.sent, sent[0])
@@ -152,26 +154,29 @@ def rank_program(g, core, T, topo):
 
     V, S = g.vector, g.scalar
     near = topo.engines(core, via_s[0])
+    spare = [e for e in near if e not in eng]
     slots = [((me - r - 1) % N, ways(T, topo, r)[3]) for r in range(N) if r != me]
     got_q = sum(len(eng) // 4 if x in own else len(eng) for x, own in slots)
-    got_n = sum(len(eng) // 2 if x in own[2:] else len(eng) for x, own in slots)
-    got_s = 2 * 2 * len(eng)
+    got_n = sum(len(eng) // 2 if x in own[:2] else len(eng) for x, own in slots)
+    got_s = (N - 1) * len(eng) // 2
 
     def hop(i, first, codes, scales):
         st, w, lnd, h = hops[i]
         oq, os_ = T["out%sq" % h], T["out%ss" % h]
         wait("g", *scales)
-        send(*[(os_[:, first + 3 * st * j:first + 3 * st * j + 2 * st + w], T["via%ss" % h][:], [c], es, "v_" + h)
-               for j, (c, es) in enumerate(zip(via_s, deal(near, 2)))])
+        feeds = [(os_[:, first + 2 * st * j:first + 2 * st * j + st + w], T["via%ss" % h][:], [c], es, "v_" + h)
+                 for j, (c, es) in enumerate(zip(via_s, deal(near, 2) + [near]))]
+        send(*feeds[:2])
+        send(feeds[2])
         wait("g", *codes)
         blk = [oq[:, first + st * x:first + st * x + w].bitcast(u8) for x in range(N - 1)]
-        send(*[(blk[x], T["via%sq" % h][:].bitcast(u8), [via_q[x]], es, "v_" + h) for x, es in zip(via_q, deal(near, 2))])
-        send(*[(blk[x], T["land%sq" % h][:, lnd[x]:lnd[x] + w].bitcast(u8), [peers[x]], es, "a_c" + h)
+        send(*[(blk[x], T["via%sq" % h][:].bitcast(u8), [via_q[x]], es, "v_" + h) for x, es in zip(via_q, deal(spare, 2))],
+             *[(blk[x], T["land%sq" % h][:, lnd[x]:lnd[x] + w].bitcast(u8), [peers[x]], es, "a_c" + h)
                for x, es in zip(direct, deal(eng, 4))])
 
-    rd = dma("y", "d_rd", T.rd[:], T.to[:])
     for i in range(8):
         tw = dma("sy"[i % 2], "d_tw", T.tw[16 * i:16 * i + 16, :], T.to[:])
+    rd = dma("s", "d_rd", T.rd[:], T.to[:])
     xl = dma("y", "d_x", T.xt[:], T.x[:])
     own = dma("s", "d_own", T.lr[me], T.to[:])
     wl = dma("s", "d_w", T.wt[:], T.w[:])
@@ -179,11 +184,11 @@ def rank_program(g, core, T, topo):
     flag = dict(allow_small_or_imprecise_dtypes=True)
     k_ta = op("g", lambda: g.iota(T.ta[:], [[1, 11], [0, 3]], 0, 0, **flag))
     k_ic = op("g", lambda: g.iota(T.ic[:], [[0, 2], [1, 16]], 0, 0, **flag))
-    k_ji = op("g", lambda: g.iota(T.ji[:], [[16, 17], [0, 2]], 0, 0, **flag))
+    k_ji = op("g", lambda: g.iota(T.ji[:], [[16, 17], [0, 2]], -20, 0, **flag))
     k_tb = op("g", lambda: g.iota(T.tb[:], [[16, 2], [0, 16]], 0, 0, **flag))
     k_cv = op("g", lambda: g.iota(T.cv[:], [[32, 8], [1, 16]], 0, 0, **flag))
     wait("g", rd)
-    raw = eng[:1]
+    raw = eng
     send((T.rd[:], T.lr[me], peers, raw, "a_raw"))
 
     op("v", lambda: V.memset(T.dm[:, 0:1], -255.0))
@@ -192,10 +197,12 @@ def rank_program(g, core, T, topo):
     k_td3 = op("v", lambda: V.transpose(T.td3[:], T.ta[:, 0:32]), k_ta)
     k_mem = op("v", lambda: V.memset(T.rst[:, 0:C:32], 0.0), k_rst)
     pd, p15, odd = T.td3[:, 0:1], T.tdc[:, 0:1], T.tdb[:, 0:1]
-    k_win2 = op("v", lambda: V.tensor_scalar(T.win2[:], T.ic[:, 0:16], pd, None, A.is_lt), k_td3, k_ic)
+    k_tdc = op("v", lambda: V.transpose(T.tdc[:], T.ic[:]), k_ic)
+    k_win2 = op("v", lambda: V.tensor_scalar(T.win2[:], T.ic[:, 0:16], pd, None, A.is_lt), k_td3)
     k_win = op("v", lambda: V.tensor_scalar(T.win[:], T.ic[:, 0:16], pd, 256.0, A.is_equal, A.mult))
-    k_tdc = op("v", lambda: V.transpose(T.tdc[:], T.ic[:]))
     k_wme = op("v", lambda: V.tensor_scalar(T.wme[:], T.ic[:, 0:16], float(me), None, A.is_equal))
+    qc = [float(3 - x + 7 * land1_at(x)) for x in direct + list(via_q) + [N - 1]]
+    k_qc = [op("v", lambda: V.memset(T.qc[:, a:a + 1], qc[a])) for a in range(4)][-1:]
     k_tdb = op("v", lambda: V.transpose(T.tdb[:], T.tb[:]), k_tb)
 
     def fill(out, value):
@@ -203,106 +210,124 @@ def rank_program(g, core, T, topo):
         src = T.ic[:, 0:n] if n <= 32 else T.rst[:, 0:n]
         return op("s", lambda: S.activation(out, src, AF.Identity, bias=float(value), scale=0.0), k_ic, k_mem)
 
+    fill(T.qc[:, 4:5], qc[4])
+    fill(T.qc[:, 5:6], qc[5])
     k_jf = op("s", lambda: S.activation(T.jf[:], T.ji[:], AF.Identity, bias=p15), k_tdc, k_ji)
-    k_jm = op("v", lambda: V.tensor_scalar(T.jm[:], T.jf[:], -20.0, 1.0 / P1, A.add, A.mult), k_jf)
-    k_ja = op("s", lambda: S.activation(T.ja[:], T.jf[:], AF.Identity, bias=-13.0, scale=7.0), k_jf)
-    k_dup = op("v", lambda: V.tensor_copy(T.dup[:], T.jf[:, 0:32]))
-    for a, b in ((0, 3), (3, 6), (6, 7)):
-        k_qc = op("s", lambda: S.activation(T.qc[:, a:b], T.ic[:, a:b], AF.Identity, scale=-1.0 - 7 * P1,
-                                            bias=3.0 + 7 * (land1_at(a) + P1 * a)))
-    k_mg = fill(T.mg[:], -R23)
+    k = op("s", lambda: S.activation(T.jm[:], T.jf[:], AF.Identity, bias=R23, scale=1.0 / P1), k_jf)
+    k_qc.append(fill(T.qc[:, 6:7], qc[6]))
+    k = op("s", lambda: S.activation(T.ja[:], T.jm[:], AF.Identity, bias=-R23), k)
+    k_jb = op("s", lambda: S.activation(T.jb[:], T.ja[:], AF.Identity, bias=127.0 / 7, scale=(1 - 7 * P1) / 7), k)
+
+    k_dup = op("v", lambda: V.tensor_scalar(T.dup[:], T.jf[:, 0:32], 20.0, None, A.add), k_jf)
 
     k_td = op("v", lambda: V.tensor_scalar(T.td16[:], T.tw[:], -127.5, 1.0 / C, A.add, A.mult), tw)
     bm, nm = T.bn[:, 0:1], T.bn[:, 1:2]
     k_b = op("s", lambda: S.activation(T.jk[:], T.win2[:].indirect(T.td16[:]), AF.Identity, accum_out=bm), k_td, k_win2)
-    k_jb = op("v", lambda: V.tensor_scalar(T.jb[:], T.jm[:], float(1 - 7 * P1), None, A.mult), k_jm)
-    k_mk = op("v", lambda: V.tensor_copy(T.mk[:], T.win[:].indirect(T.td16[:])), k_td, k_win)
+    H = C // 2
+    half = [slice(0, H), slice(H, C)]
+    k_mk = [op("v", lambda: V.tensor_copy(T.mk[:, half[i]], T.win[:].indirect(T.td16[:, 8 * i:8 * i + 8])), k_td, k_win)
+            for i in range(2)]
     k_nm = op("s", lambda: S.activation(T.jn[:], T.mk[:], AF.Identity, bias=3.0 / 7 / C, scale=1.0 / 7 / 256,
-                                        accum_out=nm), k_mk)
-    k_jc = op("v", lambda: V.tensor_tensor(T.jc[:], T.ja[:], T.jb[:], A.add), k_jb, k_ja)
-    k_dm = op("v", lambda: V.tensor_scalar(T.dm[:, 1:C], T.mk[:, 0:C - 1], -255.0 / 256, None, A.mult), k_mk)
-    k_sig = op("v", lambda: V.tensor_copy(T.sig[:], T.jc[:]), k_jc)
-    k_cc = op("v", lambda: V.tensor_tensor_scan(T.cc[:], T.mk[:], T.dm[:], bm, A.add, A.add), k_dm, k_b)
-    k_xx = op("v", lambda: V.transpose(T.xx[:], T.cc[:]), k_cc)
-    k_xc = op("v", lambda: V.tensor_tensor_scan(T.xc[:], T.rst[:], T.xx[:], 0.0, A.mult, A.max), k_xx, k_mem)
-    k_s = op("v", lambda: V.tensor_copy(T.s16[:], T.xc[:, 31:C:32]), k_xc)
-    c_v, c_w, c_7, c_u = (T.co[:, i:4 * N:4] for i in range(4))
-    k_u = op("s", lambda: S.activation(c_u, T.qc[:, 0:N], AF.Identity, bias=bm), k_b, k_qc)
-    k_c7 = op("s", lambda: S.activation(c_7, T.mg[:, 0:N], AF.Identity, bias=nm, scale=-1.0), k_nm, k_mg)
+                                        accum_out=nm), k_mk[1])
+    k_dm = [op("v", lambda: V.tensor_scalar(T.dm[:, a + 1:b + 1], T.mk[:, a:b], -255.0 / 256, None, A.mult), k_mk[i])
+            for i, (a, b) in enumerate(((0, H), (H, C - 1)))]
+    k_c0 = op("v", lambda: V.tensor_tensor_scan(T.cc[:, 0:H], T.mk[:, 0:H], T.dm[:, 0:H], bm, A.add, A.add), k_dm[0], k_b)
+    k_jc = op("v", lambda: V.tensor_tensor(T.jc[:], T.jf[:], T.jb[:], A.add), k_jb)
+    k_c1 = op("v", lambda: V.tensor_tensor_scan(T.cc[:, H:C], T.mk[:, H:C], T.dm[:, H:C], T.cc[:, H - 1:H], A.add, A.add),
+              k_dm[1], k_c0)
+    k_xx = [op("v", lambda: V.transpose(T.xx[:, h], T.cc[:, h]), k) for h, k in zip(half, (k_c0, k_c1))]
+    k_xc = [op("v", lambda: V.tensor_tensor_scan(T.xc[:, h], T.rst[:, h], T.xx[:, h], 0.0, A.mult, A.max), k, k_mem)
+            for h, k in zip(half, k_xx)]
+    k_sig = op("v", lambda: V.tensor_scalar(T.sig[:], T.jc[:], 7.0, None, A.mult), k_jc)
+    k_s = op("v", lambda: V.tensor_copy(T.s16[:], T.xc[:, 31:C:32]), k_xc[1])
+    c_v, c_w, c_u = (T.co[:, i:3 * N:3] for i in range(3))
+    k_u = op("s", lambda: S.activation(c_u, T.qc[:, 0:N], AF.Identity, bias=bm), k_b, *k_qc)
+    k_c7 = op("s", lambda: S.activation(T.bn[:, 2:3], nm, AF.Identity, bias=R23), k_nm)
     op("s", lambda: S.activation(c_v, c_u, AF.Identity, bias=R23, scale=1.0 / 7), k_u)
-    k_co = op("s", lambda: S.activation(c_w, c_u, AF.Identity, bias=T.co[:, 2:3], scale=1.0 / 7), k_c7)
+    k_co = op("s", lambda: S.activation(c_w, c_u, AF.Identity, bias=T.bn[:, 2:3], scale=1.0 / 7), k_c7)
     k_cvb = op("s", lambda: S.activation(T.cvb[:], T.cv[:], AF.Identity, bias=odd), k_cv, k_tdb)
     k_sc = op("v", lambda: V.tensor_copy(T.inv[:].indirect(T.s16[:]), T.cvb[:]), k_s, k_cvb, k_inv)
+    op("v", lambda: V.quantize_mx(T.xq[:, 0:128], T.xs[:, 0:128], T.xt[:, 0:512]), xl)
     k_vw = fill(T.vw[:, C * me:C * me + C], -4096)
+    fp, rx = T.zz[:, 0:32], 32
+    k_zz = fill(T.zz[:], 0)
+    k_r7 = fill(T.rst7[:], 1)
 
     k_ga = op("s", lambda: S.activation(T.gg[:, 0:CA], T.inv[:].indirect(T.sig[:, 0:CA // 16]), AF.Copy), k_sc, k_sig)
     k_gb = op("v", lambda: V.tensor_copy(T.gg[:, CA:448], T.inv[:].indirect(T.sig[:, CA // 16:28])), k_sc, k_sig)
-    k_xq = op("v", lambda: V.quantize_mx(T.xq[:], T.xs[:], T.xt[:]), xl)
-    k_yy = op("v", lambda: V.transpose(T.yy[:, 0:448], T.gg[:, 0:448]), k_ga, k_gb)
+    k_xq = op("v", lambda: V.quantize_mx(T.xq[:, 128:256], T.xs[:, 128:256], T.xt[:, 512:1024]))
     k_gc = op("s", lambda: S.activation(T.gg[:, 448:544], T.inv[:].indirect(T.sig[:, 28:34]), AF.Copy))
-    k_lf = op("v", lambda: V.tensor_tensor(T.lf[:, 0:14], T.yy[:, 0:448:32], T.yy[:, 16:448:32], A.add), k_yy)
-    k_yz = op("v", lambda: V.transpose(T.yy[:, 448:544], T.gg[:, 448:544]), k_gc)
-    k_l1 = op("v", lambda: V.tensor_copy(T.lst1[:, 0:14], T.lf[:, 0:14]), k_lf)
-    k_lg = op("v", lambda: V.tensor_tensor(T.lf[:, 14:17], T.yy[:, 448:544:32], T.yy[:, 464:544:32], A.add), k_yz)
+    k = op("s", lambda: S.activation(T.pa[:, 0:1], pd, AF.Identity, bias=p15, scale=-3.0))
+    k_r7 = op("s", lambda: S.activation(T.rst7[:, 0:224:7], T.ic[:], AF.Copy, scale=0.0), k_r7)
+    k = op("s", lambda: S.activation(T.pa[:, 1:2], T.pa[:, 0:1], AF.Identity, bias=odd), k)
+    k_me = op("s", lambda: S.activation(mine, T.co[:, 3 * N - 3:3 * N], AF.Copy), k_co)
+    k_pa = op("s", lambda: S.activation(T.pa[:, 2:3], T.pa[:, 1:2], AF.Identity, scale=16.0), k)
 
-    wait("g", k_co)
-    told = [T.co[:, 4 * x:4 * x + 4] for x in range(N)]
-    send(*[(told[x], T.via0[:], [c], es, "v_cnt")
-           for x, c, es in zip(direct[:2] + list(via_q), via_s + list(via_q.values()), deal(near, 4))])
-    send(*[(told[x], mine, [peers[x]], es, "a_cnt") for x, es in zip(direct[2:], deal(eng, 2))])
+    def wrap(a, b, step, dep):
+        if step == 0:
+            return op("v", lambda: V.transpose(T.yy[:, 32 * a:32 * b], T.gg[:, 32 * a:32 * b]), dep)
+        if step == 1:
+            return op("v", lambda: V.tensor_tensor(T.lf[:, a:b], T.yy[:, 32 * a:32 * b:32], T.yy[:, 32 * a + 16:32 * b:32],
+                                                   A.add), dep)
+        return op("v", lambda: V.tensor_copy(T.lst1[:, a:b], T.lf[:, a:b]), dep)
 
-    def pick(lst, a, b, oq, os_, q, s, for_q, for_s):
-        parts = [(slice(0, 16 * a), lst[:, 0:a]), (slice(16 * a, 16 * b), lst[:, a:b])]
-        ks = [op("s", lambda: S.activation(os_[:, parts[0][0]], s[:].indirect(parts[0][1]), AF.Copy), *for_s),
-              op("v", lambda: V.tensor_copy(os_[:, parts[1][0]], s[:].indirect(parts[1][1])), *for_s)]
-        kq = [op("v", lambda: V.tensor_copy(oq[:, c].bitcast(u32), q[:].bitcast(u32).indirect(o)), *for_q)
-              for c, o in parts]
-        return kq, ks
-
-    la = T.lst1[:, 14:17]
-    hop(0, 2, *pick(T.lst1, 8, 14, T.out1q, T.out1s, T.xq, T.xs, [], [k_l1, k_xq]))
-    k_vl = op("g", lambda: g.iota(T.vl[:], [[0, C]], 0, 0, **flag))
+    k_lv, k_ls = k_gb, k_ga
+    for step in range(3):
+        k_lv = wrap(CA // 32, 14, step, k_lv)
+        k_ls = wrap(0, CA // 32, step, k_ls)
 
     dma("y", "d_tr", T.tr[112:128, :], T.to[:])
     tr = dma("y", "d_tr", T.tr[0:112, :], T.lr[:], own, ("a_raw", 6 * len(raw)))
+    k_t3 = []
 
-    k_lo = op("v", lambda: V.tensor_copy(la, T.lf[:, 14:17]), k_lg)
-    k_t3 = op("v", lambda: V.tensor_scalar(T.trd16[:], T.tr[:], -127.5, 1.0 / C, A.add, A.mult), tr)
+    def dests():
+        k_t3.append(op("v", lambda: V.tensor_scalar(T.trd16[:], T.tr[:], -127.5, 1.0 / C, A.add, A.mult), tr))
+
+    wait("g", k_co)
+    send(*[(T.co[:, 3 * a:3 * a + 6], T.via0[:], [c], es, "v_cnt")
+           for a, c, es in zip((0, 2, 4, 5), via_s[:2] + list(via_q.values()), deal(near, 4))])
+    send((T.co[:, 9:12], T.via0[:, 0:3], via_s[2:], near, "v_cnt"))
+
+    def pick(lst, a, b, oq, os_, q, s, for_q, for_s, for_v, between=lambda: None):
+        parts = [(slice(16 * a, 16 * b), lst[:, a:b]), (slice(0, 16 * a), lst[:, 0:a])]
+        ks = [op("s", lambda: S.activation(os_[:, parts[1][0]], s[:].indirect(parts[1][1]), AF.Copy), *for_s),
+              op("v", lambda: V.tensor_copy(os_[:, parts[0][0]], s[:].indirect(parts[0][1])), *for_v)]
+        between()
+        kq = [op("v", lambda: V.tensor_copy(oq[:, c].bitcast(u32), q[:].bitcast(u32).indirect(o)), *for_q, *d)
+              for (c, o), d in zip(parts, ([], for_s))]
+        return kq, ks
+
+    la = T.lst1[:, 14:17]
+    hop(0, 2, *pick(T.lst1, 8, 14, T.out1q, T.out1s, T.xq, T.xs, [], [k_ls, k_xq], [k_lv, k_xq], dests))
+    k_vl = op("g", lambda: g.iota(T.vl[:], [[0, C]], 0, 0, **flag))
+
+    k_mk3 = op("s", lambda: S.activation(T.mk3[:], T.wme[:].indirect(T.trd16[:]), AF.Copy), *k_t3, k_wme)
+    k_pos = op("s", lambda: S.activation(T.pos[:], T.ic[:], AF.Identity, bias=T.pa[:, 2:3]), k_pa)
+    k_low = op("s", lambda: S.activation(T.low[:], T.pos[:], AF.Identity, bias=-128.0 - R23), k_pos)
+    k_lo = wrap(14, 17, 0, k_gc)
     kb = op("v", lambda: V.tensor_copy(T.tr16[:], T.tr[:]))
-    k_mk3 = op("s", lambda: S.activation(T.mk3[:], T.wme[:].indirect(T.trd16[:]), AF.Copy), k_t3, k_wme)
-    k_b1 = op("s", lambda: S.activation(T.land1s[:, OWN1:OWN1 + 48], T.xs[:].indirect(la), AF.Copy), k_lo)
-    k_a1 = op("v", lambda: V.tensor_copy(T.land1q[:, OWN1:OWN1 + 48].bitcast(u32), T.xq[:].bitcast(u32).indirect(la)),
-              k_lo)
-    k_wq = op("v", lambda: V.quantize_mx(T.wq[:], T.ws[:], T.wt[:]), wl)
+    k_lo = wrap(14, 17, 1, k_lo)
     k = op("v", lambda: V.tensor_tensor_scan(T.kv[:], T.mk3[:], T.mk3[:], 0.0, A.add, A.max), k_mk3)
+    cn = ("a_cnt", got_n)
+    k_jj = op("v", lambda: V.tensor_tensor(T.jj[:, 1:N], T.cb[:, 4:4 * N:4], T.cb[:, 1:4 * N - 4:4], A.subtract), cn, k_me)
+    k_rx = op("v", lambda: V.tensor_tensor_scan(T.zz[:, rx + 1:rx + 8], T.cb[:, 1:4 * N:4], T.cb[:, 0:4 * N:4], 0.0,
+                                                A.add, A.subtract), k_zz)
+    k_lo = wrap(14, 17, 2, k_lo)
     k_v = op("v", lambda: V.tensor_copy(T.vw[:].indirect(T.tr16[:]), T.kv[:]), k, kb, k_vw)
-    for i in range(4):
-        vl = dma("y", "d_vl", T.vl[32 * i:32 * i + 4 * N:4, :], T.vw[0:16 * N:16, C * me:C * me + C], k_v, k_vl)
+    k_b1 = op("s", lambda: S.activation(T.land1s[:, OWN1:OWN1 + 48], T.xs[:].indirect(la), AF.Copy), k_lo)
 
-    fp, rx = T.zz[:, 0:32], 32
-    k_me = op("s", lambda: S.activation(mine, told[N - 1], AF.Copy), k_co)
-    k = op("s", lambda: S.activation(T.pa[:, 0:1], pd, AF.Identity, bias=p15, scale=-3.0))
-    k_zz = fill(T.zz[:], 0)
-    k = op("s", lambda: S.activation(T.pa[:, 1:2], T.pa[:, 0:1], AF.Identity, bias=odd), k)
-    k_r7 = fill(T.rst7[:], 1)
-    k = op("s", lambda: S.activation(T.pa[:, 2:3], T.pa[:, 1:2], AF.Identity, scale=16.0), k)
-    k_r7 = op("s", lambda: S.activation(T.rst7[:, 0:224:7], T.ic[:], AF.Copy, scale=0.0), k_r7)
-    k_pos = op("s", lambda: S.activation(T.pos[:], T.ic[:], AF.Identity, bias=T.pa[:, 2:3]), k)
+    k_g0 = op("s", lambda: S.activation(T.gr[:, 0:224:7], T.low[:], AF.Identity, bias=T.cb[:, 0:1]), k_low, cn)
     fill(T.hz[:, 1:64:4], -R23)
-    for i, m in enumerate((0, 1, -7, S2)):
+    for i, m in enumerate((0, 1, -7, P2)):
         k_hm = fill(T.hm[:, i:64:4], m)
-
-    k_jj = op("v", lambda: V.tensor_tensor(T.jj[:, 1:N], T.cb[:, 4:4 * N:4], T.cb[:, 1:4 * N - 4:4], A.subtract),
-              ("a_cnt", got_n), k_me)
-    k_rx = op("v", lambda: V.tensor_tensor_scan(T.zz[:, rx + 1:rx + 8], T.cb[:, 2:4 * N:4], T.mg[:, 0:N], 0.0,
-                                                A.add, A.add), k_zz)
-    op("v", lambda: V.tensor_scalar(T.gr[:, 0:224:7], T.pos[:], T.cb[:, 0:1], -128.0 - R23, A.add, A.add), k_pos)
+    for i in range(4):
+        vl = dma("ys"[i % 2], "d_vl", T.vl[32 * i:32 * i + 4 * N:4, :], T.vw[0:16 * N:16, C * me:C * me + C], k_v, k_vl)
     for r in range(1, N):
         k_gr = op("v", lambda: V.tensor_scalar(T.gr[:, r:224:7], T.pos[:], T.zz[:, rx + r:rx + r + 1], T.jj[:, r:r + 1],
-                                               A.is_ge, A.mult), k_jj, k_rx)
+                                               A.is_ge, A.mult), k_jj, k_rx, k_pos)
     k_f2 = op("v", lambda: V.tensor_scalar(T.f2[:, 0:N], T.zz[:, rx:rx + N], 7.0 * U, float(SHIFT - U), A.mult, A.add))
-    k = op("v", lambda: V.tensor_tensor_scan(T.gs[:], T.rst7[:], T.gr[:], 0.0, A.mult, A.add), k_gr, k_r7)
-    k_f = op("v", lambda: V.tensor_tensor(T.zz[:, 0:4 * N:4], T.cb[:, 3:4 * N:4], T.f2[:, 0:N], A.add), k_f2)
+    k = op("v", lambda: V.tensor_tensor_scan(T.gs[:], T.rst7[:], T.gr[:], 0.0, A.mult, A.add), k_gr, k_r7, k_g0)
+    k_f = op("v", lambda: V.tensor_tensor(T.zz[:, 0:4 * N:4], T.cb[:, 2:4 * N:4], T.f2[:, 0:N], A.add), k_f2)
     k = op("v", lambda: V.transpose(T.l2t[:], T.gs[:, 6:224:7]), k)
     k_ft = op("v", lambda: V.transpose(T.ft[:], fp), k_f)
     e = 3 * (N - 1 - me)
@@ -310,19 +335,25 @@ def rank_program(g, core, T, topo):
     if e:
         op("v", lambda: V.tensor_scalar(T.lst2[:, 0:e], T.l2t[:, 3 * (me + 1):21], *top), k)
     k_l2 = op("v", lambda: V.tensor_scalar(T.lst2[:, e:21], T.l2t[:, 0:3 * (me + 1)], *top), k)
+    k_a1 = op("v", lambda: V.tensor_copy(T.land1q[:, OWN1:OWN1 + 48].bitcast(u32), T.xq[:].bitcast(u32).indirect(la)),
+              k_lo)
 
     la = T.lst2[:, 18:21]
     hop(1, 0, *pick(T.lst2, 10, 18, T.out2q, T.out2s, T.land1q, T.land1s, [k_a1, ("a_c1", got_q)],
-                    [k_l2, k_b1, ("a_s1", got_s)]))
-    k_a2 = op("v", lambda: V.tensor_copy(T.land2q[:, 6 * S2:7 * S2].bitcast(u32),
-                                         T.land1q[:].bitcast(u32).indirect(la)))
+                    [k_l2, k_b1, ("a_s1", got_s)], [k_l2, k_b1, ("a_s1", got_s)]))
+
 
     kw = [op("s", lambda: S.activation(T.w3[:, 256 * i:256 * i + 256], T.vl[:].indirect(T.dup[:, 16 * i:16 * i + 16]),
                                        AF.Relu, bias=T.ft[:, 3 * me:3 * me + 1], scale=float(U)), vl, k_ft, k_dup)
           for i in range(2)]
-    k_b2 = op("s", lambda: S.activation(T.land2s[:, 6 * S2:7 * S2], T.land1s[:].indirect(la), AF.Copy))
+    k_b2 = op("s", lambda: S.activation(T.land2s[:, L2W - 48:L2W], T.land1s[:].indirect(la), AF.Copy))
     for i in range(2):
         k = op("v", lambda: V.transpose(T.y3[:, 256 * i:256 * i + 256], T.w3[:, 256 * i:256 * i + 256]), kw[i])
+        if i == 0:
+            k_a2 = op("v", lambda: V.tensor_copy(T.land2q[:, L2W - 48:L2W].bitcast(u32),
+                                                 T.land1q[:].bitcast(u32).indirect(la)))
+        else:
+            k_wq = op("v", lambda: V.quantize_mx(T.wq[:], T.ws[:], T.wt[:]), wl)
         k = op("v", lambda: V.tensor_tensor_scan(T.fo[:, 64 * i:64 * i + 64], T.rst[:, 0:C:4],
                                                  T.y3[:, 256 * i:256 * i + 256:4], 0.0, A.mult, A.add), k)
     z = T.fo[:, 7:128:8]
@@ -330,7 +361,7 @@ def rank_program(g, core, T, topo):
     op("v", lambda: V.tensor_copy(T.hz[:, 2:64:4], z))
     k = op("v", lambda: V.tensor_scalar(T.hz[:, 3:64:4], z, 1.0 / (7 * U), R23, A.mult, A.add))
     k = op("v", lambda: V.tensor_tensor_scan(T.ho[:], T.hm[:], T.hz[:], 0.0, A.mult, A.add), k, k_hm)
-    k_l3 = op("v", lambda: V.tensor_scalar(T.lst3[:], T.ho[:, 3:64:4], 3.0 * S2 - 1 - R23, None, A.add), k)
+    k_l3 = op("v", lambda: V.tensor_scalar(T.lst3[:], T.ho[:, 3:64:4], L2 + 3.0 * P2 - 1 - R23, None, A.add), k)
 
     c2, s2 = ("a_c2", got_q), ("a_s2", got_s)
     cols = [slice(128 * i, 128 * i + 128) for i in range(2)]

from concourse.bass import DstId, RemoteDMATransfer
from concourse.mybir import dt, AluOpType, ActivationFunctionType

N, C = 7, 256
P1, P2, S2 = 37, 42, 48
OWN1 = 112
L1W = OWN1 + 48 + 3 * P1
L2 = 4
L2W = L2 + 6 * P2 + 48
U = 4096
SHIFT = 7 * U - 13300
CA = 256
R23 = 12582912.0

F32, BF, I32, U16, CODES, PLANE = "float32", "bfloat16", "int32", "uint16", "float8_e4m3fn_x4", "uint8"
SCRATCH = {
    "ta": ("sbuf", [128, 33], F32), "td3": ("sbuf", [128, 32], F32),
    "tb": ("sbuf", [128, 32], F32), "tdb": ("sbuf", [128, 32], F32), "tdc": ("sbuf", [128, 32], F32),
    "ic": ("sbuf", [128, 32], F32), "win": ("sbuf", [128, 16], BF), "win2": ("sbuf", [128, 16], BF),
    "wme": ("sbuf", [128, 16], BF), "rst": ("sbuf", [128, C], BF), "rst7": ("sbuf", [128, 7 * 32], BF),
    "cv": ("sbuf", [128, 128], F32), "cvb": ("sbuf", [128, 128], BF),
    "ji": ("sbuf", [128, 34], F32), "jm": ("sbuf", [128, 34], F32), "jf": ("sbuf", [128, 34], F32),
    "ja": ("sbuf", [128, 34], F32), "jb": ("sbuf", [128, 34], F32), "jc": ("sbuf", [128, 34], F32),
    "sig": ("sbuf", [128, 34], U16), "dup": ("sbuf", [128, 32], U16),
    "pa": ("sbuf", [128, 4], F32), "pos": ("sbuf", [128, 32], F32), "low": ("sbuf", [128, 32], F32),
    "qc": ("sbuf", [128, 8], F32), "hm": ("sbuf", [128, 64], F32),
    "tw": ("sbuf", [128, 16], I32), "td16": ("sbuf", [128, 16], U16),
    "mk": ("sbuf", [128, C], BF), "jk": ("sbuf", [128, C], BF), "jn": ("sbuf", [128, C], F32),
    "dm": ("sbuf", [128, C], BF), "cc": ("sbuf", [128, C], BF),
    "xx": ("sbuf", [128, C], BF), "xc": ("sbuf", [128, C], BF),
    "s16": ("sbuf", [128, 8], U16), "inv": ("sbuf", [128, 272], BF), "gg": ("sbuf", [128, 544], BF),
    "yy": ("sbuf", [128, 544], BF), "lf": ("sbuf", [128, 18], F32), "lst1": ("sbuf", [128, 18], U16),
    "bn": ("sbuf", [128, 4], F32), "co": ("sbuf", [128, 3 * N], F32), "cb": ("sbuf", [128, 4 * N], F32),
    "zz": ("sbuf", [128, 40], F32),
    "jj": ("sbuf", [128, 8], F32), "gr": ("sbuf", [128, 7 * 32], BF), "gs": ("sbuf", [128, 7 * 32], BF),
    "l2t": ("sbuf", [128, 32], BF), "lst2": ("sbuf", [128, 22], U16),
    "rd": ("dram", [128, 2], I32), "lr": ("dram", [N, 128, 2], I32),
    "tr": ("sbuf", [128, 16], I32), "tr16": ("sbuf", [128, 16], U16),
    "trd16": ("sbuf", [128, 16], U16), "mk3": ("sbuf", [128, C], BF), "kv": ("sbuf", [128, C], BF),
    "vw": ("sbuf", [128, N * C], BF), "vl": ("sbuf", [128, C], BF), "f2": ("sbuf", [128, 8], F32),
    "ft": ("sbuf", [128, 32], F32), "w3": ("sbuf", [128, 512], F32), "y3": ("sbuf", [128, 512], F32),
    "fo": ("sbuf", [128, 128], F32), "hz": ("sbuf", [128, 64], F32), "ho": ("sbuf", [128, 64], F32),
    "lst3": ("sbuf", [128, 16], U16),
    "xt": ("sbuf", [128, 4 * C], BF), "wt": ("sbuf", [128, 512], BF),
    "xq": ("sbuf", [128, C], CODES), "xs": ("sbuf", [128, C], PLANE),
    "wq": ("sbuf", [128, 128], CODES), "ws": ("sbuf", [128, 128], PLANE),
    "out1q": ("sbuf", [128, 224], CODES), "out1s": ("sbuf", [128, 224], PLANE),
    "land1q": ("sbuf", [128, L1W], CODES), "land1s": ("sbuf", [128, L1W], PLANE),
    "out2q": ("sbuf", [128, 6 * S2], CODES), "out2s": ("sbuf", [128, 6 * S2], PLANE),
    "land2q": ("sbuf", [128, L2W], CODES), "land2s": ("sbuf", [128, L2W], PLANE),
    "fq": ("sbuf", [128, C], CODES), "fs": ("sbuf", [128, C], PLANE),
    "ps": ("psum", [128, 1024], F32), "ys": ("sbuf", [128, C], F32),
    "via0": ("sbuf", [128, 6], F32),
    "via1q": ("sbuf", [128, P1], CODES), "via1s": ("sbuf", [128, 2 * P1], PLANE),
    "via2q": ("sbuf", [128, P2], CODES), "via2s": ("sbuf", [128, S2 + P2], PLANE),
}
SEMAPHORES = ["ev", "es", "eg", "et",
              "d_rd", "d_tw", "d_x", "d_w", "d_own", "d_tr", "d_vl", "d_y0", "d_y1",
              "a_raw", "a_cnt", "a_c1", "a_s1", "a_c2", "a_s2",
              "v_cnt", "v_1", "v_2",
              "sent"]


def land1_at(x):
    return OWN1 if x == N - 1 else OWN1 + 48 + P1 * (2 - x) if x < 3 else 1 + P1 * (5 - x)


def ways(T, topo, r):
    core = T.cores[r]
    peers = [T.cores[(r + 1 + x) % N] for x in range(N - 1)]
    free = sorted((c for c in topo.cores_of(core) if c != core), key=lambda c: topo.die(c) == topo.die(core))
    scales = [c for c in free if all(topo.may_write(c, p) for p in peers)][:3]
    rest = [c for c in free if topo.die(c) == topo.die(core) and c not in scales]
    codes = {}
    for x, p in enumerate(peers):
        if len(codes) < 2 and topo.may_write(rest[len(codes)], p):
            codes[x] = rest[len(codes)]
    return peers, scales, codes, [x for x in range(N - 1) if x not in codes]


def rank_program(g, core, T, topo):
    host = [T.rank_of(c) for c in topo.cores_of(core) if T.rank_of(c) is not None]
    if not host:
        return
    me = host[0]
    peers, via_s, via_q, direct = ways(T, topo, me)
    eng = [e for e in topo.engines(core, peers[0]) if all(e in topo.engines(core, p) for p in peers)]
    u32, u8 = dt.uint32, dt.uint8
    sent = [0]

    def send(*transfers):
        def dst(p):
            rid, pid, _ = topo.addr(p)
            return DstId(rid=rid, pnc=pid)
        g.remote_dma_fused([RemoteDMATransfer(dst_ids=[dst(p) for p in to], dma_engine_mask=sum(1 << e for e in es),
                                              remote_sem=T.sem[sem], srcs=[s], dsts=[d] * len(to))
                            for s, d, to, es, sem in transfers], local_sem=T.sem.sent)
        sent[0] += sum(len(t[3]) for t in transfers)

    def deal(es, k):
        return [es[i * len(es) // k:(i + 1) * len(es) // k] for i in range(k)]

    hops = [(P1, P1, [land1_at(x) for x in range(N - 1)], "1"),
            (S2, P2, [L2 + P2 * (N - 2 - x) for x in range(N - 1)], "2")]
    mine = T.cb[:, 4 * me:4 * me + 3]

    if core != T.cores[me]:
        if core not in via_s and core not in via_q.values():
            return
        fed = len(topo.engines(T.cores[me], core))
        g.wait_ge(T.sem.v_cnt, fed if core == via_s[2] else fed // 4)
        if core in via_s:
            i = via_s.index(core)
            told = [direct[0:2], direct[2:3], direct[3:4]][i]
            send(*[(T.via0[:, 3 * j:3 * j + 3], mine, [peers[x]], es, "a_cnt")
                   for j, (x, es) in enumerate(zip(told, deal(eng, len(told))))])
            for st, w, lnd, h in hops:
                g.wait_ge(T.sem["v_" + h], fed // 2 if i < 2 else fed)
                send(*[(T["via%ss" % h][:, st * j:st * j + w], T["land%ss" % h][:, lnd[x]:lnd[x] + w], [peers[x]], es,
                        "a_s" + h) for j, (x, es) in enumerate(zip((2 * i, 2 * i + 1), deal(eng, 2)))])
        else:
            x = [x for x in via_q if via_q[x] == core][0]
            send((T.via0[:, 0:3], mine, [peers[x]], eng, "a_cnt"))
            for st, w, lnd, h in hops:
                g.wait_ge(T.sem["v_" + h], fed // 4)
                send((T["via%sq" % h][:].bitcast(u8), T["land%sq" % h][:, lnd[x]:lnd[x] + w].bitcast(u8), [peers[x]], eng,
                      "a_c" + h))
        g.wait_ge(T.sem.sent, sent[0])
        return

    A, AF = AluOpType, ActivationFunctionType
    queue = {"v": g.vector, "s": g.scalar, "g": g, "t": g.tensor, "y": g.sync}
    count = {}
    seen = {k: {} for k in queue}

    def wait(q, *deps):
        for sem, n in deps:
            if seen[q].get(sem, 0) < n:
                queue[q].wait_ge(T.sem[sem], n)
                seen[q][sem] = n

    def op(q, call, *deps):
        wait(q, *deps)
        sem = "e" + q
        call().then_inc(T.sem[sem], 1)
        count[sem] = count.get(sem, 0) + 1
        return (sem, count[sem])

    def dma(q, sem, out, in_, *deps):
        wait(q, *deps)
        queue[q].dma_start(out, in_).then_inc(T.sem[sem], 16)
        count[sem] = count.get(sem, 0) + 16
        return (sem, count[sem])

    V, S = g.vector, g.scalar
    near = topo.engines(core, via_s[0])
    spare = [e for e in near if e not in eng]
    slots = [((me - r - 1) % N, ways(T, topo, r)[3]) for r in range(N) if r != me]
    got_q = sum(len(eng) // 4 if x in own else len(eng) for x, own in slots)
    got_n = sum(len(eng) // 2 if x in own[:2] else len(eng) for x, own in slots)
    got_s = (N - 1) * len(eng) // 2

    def hop(i, first, codes, scales):
        st, w, lnd, h = hops[i]
        oq, os_ = T["out%sq" % h], T["out%ss" % h]
        wait("g", *scales)
        feeds = [(os_[:, first + 2 * st * j:first + 2 * st * j + st + w], T["via%ss" % h][:], [c], es, "v_" + h)
                 for j, (c, es) in enumerate(zip(via_s, deal(near, 2) + [near]))]
        send(*feeds[:2])
        send(feeds[2])
        wait("g", *codes)
        blk = [oq[:, first + st * x:first + st * x + w].bitcast(u8) for x in range(N - 1)]
        send(*[(blk[x], T["via%sq" % h][:].bitcast(u8), [via_q[x]], es, "v_" + h) for x, es in zip(via_q, deal(spare, 2))],
             *[(blk[x], T["land%sq" % h][:, lnd[x]:lnd[x] + w].bitcast(u8), [peers[x]], es, "a_c" + h)
               for x, es in zip(direct, deal(eng, 4))])

    for i in range(8):
        tw = dma("sy"[i % 2], "d_tw", T.tw[16 * i:16 * i + 16, :], T.to[:])
    rd = dma("s", "d_rd", T.rd[:], T.to[:])
    xl = dma("y", "d_x", T.xt[:], T.x[:])
    own = dma("s", "d_own", T.lr[me], T.to[:])
    wl = dma("s", "d_w", T.wt[:], T.w[:])

    flag = dict(allow_small_or_imprecise_dtypes=True)
    k_ta = op("g", lambda: g.iota(T.ta[:], [[1, 11], [0, 3]], 0, 0, **flag))
    k_ic = op("g", lambda: g.iota(T.ic[:], [[0, 2], [1, 16]], 0, 0, **flag))
    k_ji = op("g", lambda: g.iota(T.ji[:], [[16, 17], [0, 2]], -20, 0, **flag))
    k_tb = op("g", lambda: g.iota(T.tb[:], [[16, 2], [0, 16]], 0, 0, **flag))
    k_cv = op("g", lambda: g.iota(T.cv[:], [[32, 8], [1, 16]], 0, 0, **flag))
    wait("g", rd)
    raw = eng
    send((T.rd[:], T.lr[me], peers, raw, "a_raw"))

    op("v", lambda: V.memset(T.dm[:, 0:1], -255.0))
    k_rst = op("v", lambda: V.memset(T.rst[:], 1.0))
    k_inv = op("v", lambda: V.memset(T.inv[:], 0.0))
    k_td3 = op("v", lambda: V.transpose(T.td3[:], T.ta[:, 0:32]), k_ta)
    k_mem = op("v", lambda: V.memset(T.rst[:, 0:C:32], 0.0), k_rst)
    pd, p15, odd = T.td3[:, 0:1], T.tdc[:, 0:1], T.tdb[:, 0:1]
    k_tdc = op("v", lambda: V.transpose(T.tdc[:], T.ic[:]), k_ic)
    k_win2 = op("v", lambda: V.tensor_scalar(T.win2[:], T.ic[:, 0:16], pd, None, A.is_lt), k_td3)
    k_win = op("v", lambda: V.tensor_scalar(T.win[:], T.ic[:, 0:16], pd, 256.0, A.is_equal, A.mult))
    k_wme = op("v", lambda: V.tensor_scalar(T.wme[:], T.ic[:, 0:16], float(me), None, A.is_equal))
    qc = [float(3 - x + 7 * land1_at(x)) for x in direct + list(via_q) + [N - 1]]
    k_qc = [op("v", lambda: V.memset(T.qc[:, a:a + 1], qc[a])) for a in range(4)][-1:]
    k_tdb = op("v", lambda: V.transpose(T.tdb[:], T.tb[:]), k_tb)

    def fill(out, value):
        n = out.shape[1]
        src = T.ic[:, 0:n] if n <= 32 else T.rst[:, 0:n]
        return op("s", lambda: S.activation(out, src, AF.Identity, bias=float(value), scale=0.0), k_ic, k_mem)

    fill(T.qc[:, 4:5], qc[4])
    fill(T.qc[:, 5:6], qc[5])
    k_jf = op("s", lambda: S.activation(T.jf[:], T.ji[:], AF.Identity, bias=p15), k_tdc, k_ji)
    k = op("s", lambda: S.activation(T.jm[:], T.jf[:], AF.Identity, bias=R23, scale=1.0 / P1), k_jf)
    k_qc.append(fill(T.qc[:, 6:7], qc[6]))
    k = op("s", lambda: S.activation(T.ja[:], T.jm[:], AF.Identity, bias=-R23), k)
    k_jb = op("s", lambda: S.activation(T.jb[:], T.ja[:], AF.Identity, bias=127.0 / 7, scale=(1 - 7 * P1) / 7), k)

    k_dup = op("v", lambda: V.tensor_scalar(T.dup[:], T.jf[:, 0:32], 20.0, None, A.add), k_jf)

    k_td = op("v", lambda: V.tensor_scalar(T.td16[:], T.tw[:], -127.5, 1.0 / C, A.add, A.mult), tw)
    bm, nm = T.bn[:, 0:1], T.bn[:, 1:2]
    k_b = op("s", lambda: S.activation(T.jk[:], T.win2[:].indirect(T.td16[:]), AF.Identity, accum_out=bm), k_td, k_win2)
    H = C // 2
    half = [slice(0, H), slice(H, C)]
    k_mk = [op("v", lambda: V.tensor_copy(T.mk[:, half[i]], T.win[:].indirect(T.td16[:, 8 * i:8 * i + 8])), k_td, k_win)
            for i in range(2)]
    k_nm = op("s", lambda: S.activation(T.jn[:], T.mk[:], AF.Identity, bias=3.0 / 7 / C, scale=1.0 / 7 / 256,
                                        accum_out=nm), k_mk[1])
    k_dm = [op("v", lambda: V.tensor_scalar(T.dm[:, a + 1:b + 1], T.mk[:, a:b], -255.0 / 256, None, A.mult), k_mk[i])
            for i, (a, b) in enumerate(((0, H), (H, C - 1)))]
    k_c0 = op("v", lambda: V.tensor_tensor_scan(T.cc[:, 0:H], T.mk[:, 0:H], T.dm[:, 0:H], bm, A.add, A.add), k_dm[0], k_b)
    k_jc = op("v", lambda: V.tensor_tensor(T.jc[:], T.jf[:], T.jb[:], A.add), k_jb)
    k_c1 = op("v", lambda: V.tensor_tensor_scan(T.cc[:, H:C], T.mk[:, H:C], T.dm[:, H:C], T.cc[:, H - 1:H], A.add, A.add),
              k_dm[1], k_c0)
    k_xx = [op("v", lambda: V.transpose(T.xx[:, h], T.cc[:, h]), k) for h, k in zip(half, (k_c0, k_c1))]
    k_xc = [op("v", lambda: V.tensor_tensor_scan(T.xc[:, h], T.rst[:, h], T.xx[:, h], 0.0, A.mult, A.max), k, k_mem)
            for h, k in zip(half, k_xx)]
    k_sig = op("v", lambda: V.tensor_scalar(T.sig[:], T.jc[:], 7.0, None, A.mult), k_jc)
    k_s = op("v", lambda: V.tensor_copy(T.s16[:], T.xc[:, 31:C:32]), k_xc[1])
    c_v, c_w, c_u = (T.co[:, i:3 * N:3] for i in range(3))
    k_u = op("s", lambda: S.activation(c_u, T.qc[:, 0:N], AF.Identity, bias=bm), k_b, *k_qc)
    k_c7 = op("s", lambda: S.activation(T.bn[:, 2:3], nm, AF.Identity, bias=R23), k_nm)
    op("s", lambda: S.activation(c_v, c_u, AF.Identity, bias=R23, scale=1.0 / 7), k_u)
    k_co = op("s", lambda: S.activation(c_w, c_u, AF.Identity, bias=T.bn[:, 2:3], scale=1.0 / 7), k_c7)
    k_cvb = op("s", lambda: S.activation(T.cvb[:], T.cv[:], AF.Identity, bias=odd), k_cv, k_tdb)
    k_sc = op("v", lambda: V.tensor_copy(T.inv[:].indirect(T.s16[:]), T.cvb[:]), k_s, k_cvb, k_inv)
    op("v", lambda: V.quantize_mx(T.xq[:, 0:128], T.xs[:, 0:128], T.xt[:, 0:512]), xl)
    k_vw = fill(T.vw[:, C * me:C * me + C], -4096)
    fp, rx = T.zz[:, 0:32], 32
    k_zz = fill(T.zz[:], 0)
    k_r7 = fill(T.rst7[:], 1)

    k_ga = op("s", lambda: S.activation(T.gg[:, 0:CA], T.inv[:].indirect(T.sig[:, 0:CA // 16]), AF.Copy), k_sc, k_sig)
    k_gb = op("v", lambda: V.tensor_copy(T.gg[:, CA:448], T.inv[:].indirect(T.sig[:, CA // 16:28])), k_sc, k_sig)
    k_xq = op("v", lambda: V.quantize_mx(T.xq[:, 128:256], T.xs[:, 128:256], T.xt[:, 512:1024]))
    k_gc = op("s", lambda: S.activation(T.gg[:, 448:544], T.inv[:].indirect(T.sig[:, 28:34]), AF.Copy))
    k = op("s", lambda: S.activation(T.pa[:, 0:1], pd, AF.Identity, bias=p15, scale=-3.0))
    k_r7 = op("s", lambda: S.activation(T.rst7[:, 0:224:7], T.ic[:], AF.Copy, scale=0.0), k_r7)
    k = op("s", lambda: S.activation(T.pa[:, 1:2], T.pa[:, 0:1], AF.Identity, bias=odd), k)
    k_me = op("s", lambda: S.activation(mine, T.co[:, 3 * N - 3:3 * N], AF.Copy), k_co)
    k_pa = op("s", lambda: S.activation(T.pa[:, 2:3], T.pa[:, 1:2], AF.Identity, scale=16.0), k)

    def wrap(a, b, step, dep):
        if step == 0:
            return op("v", lambda: V.transpose(T.yy[:, 32 * a:32 * b], T.gg[:, 32 * a:32 * b]), dep)
        if step == 1:
            return op("v", lambda: V.tensor_tensor(T.lf[:, a:b], T.yy[:, 32 * a:32 * b:32], T.yy[:, 32 * a + 16:32 * b:32],
                                                   A.add), dep)
        return op("v", lambda: V.tensor_copy(T.lst1[:, a:b], T.lf[:, a:b]), dep)

    k_lv, k_ls = k_gb, k_ga
    for step in range(3):
        k_lv = wrap(CA // 32, 14, step, k_lv)
        k_ls = wrap(0, CA // 32, step, k_ls)

    dma("y", "d_tr", T.tr[112:128, :], T.to[:])
    tr = dma("y", "d_tr", T.tr[0:112, :], T.lr[:], own, ("a_raw", 6 * len(raw)))
    k_t3 = []

    def dests():
        k_t3.append(op("v", lambda: V.tensor_scalar(T.trd16[:], T.tr[:], -127.5, 1.0 / C, A.add, A.mult), tr))

    wait("g", k_co)
    send(*[(T.co[:, 3 * a:3 * a + 6], T.via0[:], [c], es, "v_cnt")
           for a, c, es in zip((0, 2, 4, 5), via_s[:2] + list(via_q.values()), deal(near, 4))])
    send((T.co[:, 9:12], T.via0[:, 0:3], via_s[2:], near, "v_cnt"))

    def pick(lst, a, b, oq, os_, q, s, for_q, for_s, for_v, between=lambda: None):
        parts = [(slice(16 * a, 16 * b), lst[:, a:b]), (slice(0, 16 * a), lst[:, 0:a])]
        ks = [op("s", lambda: S.activation(os_[:, parts[1][0]], s[:].indirect(parts[1][1]), AF.Copy), *for_s),
              op("v", lambda: V.tensor_copy(os_[:, parts[0][0]], s[:].indirect(parts[0][1])), *for_v)]
        between()
        kq = [op("v", lambda: V.tensor_copy(oq[:, c].bitcast(u32), q[:].bitcast(u32).indirect(o)), *for_q, *d)
              for (c, o), d in zip(parts, ([], for_s))]
        return kq, ks

    la = T.lst1[:, 14:17]
    hop(0, 2, *pick(T.lst1, 8, 14, T.out1q, T.out1s, T.xq, T.xs, [], [k_ls, k_xq], [k_lv, k_xq], dests))
    k_vl = op("g", lambda: g.iota(T.vl[:], [[0, C]], 0, 0, **flag))

    k_mk3 = op("s", lambda: S.activation(T.mk3[:], T.wme[:].indirect(T.trd16[:]), AF.Copy), *k_t3, k_wme)
    k_pos = op("s", lambda: S.activation(T.pos[:], T.ic[:], AF.Identity, bias=T.pa[:, 2:3]), k_pa)
    k_low = op("s", lambda: S.activation(T.low[:], T.pos[:], AF.Identity, bias=-128.0 - R23), k_pos)
    k_lo = wrap(14, 17, 0, k_gc)
    kb = op("v", lambda: V.tensor_copy(T.tr16[:], T.tr[:]))
    k_lo = wrap(14, 17, 1, k_lo)
    k = op("v", lambda: V.tensor_tensor_scan(T.kv[:], T.mk3[:], T.mk3[:], 0.0, A.add, A.max), k_mk3)
    cn = ("a_cnt", got_n)
    k_jj = op("v", lambda: V.tensor_tensor(T.jj[:, 1:N], T.cb[:, 4:4 * N:4], T.cb[:, 1:4 * N - 4:4], A.subtract), cn, k_me)
    k_rx = op("v", lambda: V.tensor_tensor_scan(T.zz[:, rx + 1:rx + 8], T.cb[:, 1:4 * N:4], T.cb[:, 0:4 * N:4], 0.0,
                                                A.add, A.subtract), k_zz)
    k_lo = wrap(14, 17, 2, k_lo)
    k_v = op("v", lambda: V.tensor_copy(T.vw[:].indirect(T.tr16[:]), T.kv[:]), k, kb, k_vw)
    k_b1 = op("s", lambda: S.activation(T.land1s[:, OWN1:OWN1 + 48], T.xs[:].indirect(la), AF.Copy), k_lo)

    k_g0 = op("s", lambda: S.activation(T.gr[:, 0:224:7], T.low[:], AF.Identity, bias=T.cb[:, 0:1]), k_low, cn)
    fill(T.hz[:, 1:64:4], -R23)
    for i, m in enumerate((0, 1, -7, P2)):
        k_hm = fill(T.hm[:, i:64:4], m)
    for i in range(4):
        vl = dma("ys"[i % 2], "d_vl", T.vl[32 * i:32 * i + 4 * N:4, :], T.vw[0:16 * N:16, C * me:C * me + C], k_v, k_vl)
    for r in range(1, N):
        k_gr = op("v", lambda: V.tensor_scalar(T.gr[:, r:224:7], T.pos[:], T.zz[:, rx + r:rx + r + 1], T.jj[:, r:r + 1],
                                               A.is_ge, A.mult), k_jj, k_rx, k_pos)
    k_f2 = op("v", lambda: V.tensor_scalar(T.f2[:, 0:N], T.zz[:, rx:rx + N], 7.0 * U, float(SHIFT - U), A.mult, A.add))
    k = op("v", lambda: V.tensor_tensor_scan(T.gs[:], T.rst7[:], T.gr[:], 0.0, A.mult, A.add), k_gr, k_r7, k_g0)
    k_f = op("v", lambda: V.tensor_tensor(T.zz[:, 0:4 * N:4], T.cb[:, 2:4 * N:4], T.f2[:, 0:N], A.add), k_f2)
    k = op("v", lambda: V.transpose(T.l2t[:], T.gs[:, 6:224:7]), k)
    k_ft = op("v", lambda: V.transpose(T.ft[:], fp), k_f)
    e = 3 * (N - 1 - me)
    top = (128.0, float(L1W - 1), A.add, A.min)
    if e:
        op("v", lambda: V.tensor_scalar(T.lst2[:, 0:e], T.l2t[:, 3 * (me + 1):21], *top), k)
    k_l2 = op("v", lambda: V.tensor_scalar(T.lst2[:, e:21], T.l2t[:, 0:3 * (me + 1)], *top), k)
    k_a1 = op("v", lambda: V.tensor_copy(T.land1q[:, OWN1:OWN1 + 48].bitcast(u32), T.xq[:].bitcast(u32).indirect(la)),
              k_lo)

    la = T.lst2[:, 18:21]
    hop(1, 0, *pick(T.lst2, 10, 18, T.out2q, T.out2s, T.land1q, T.land1s, [k_a1, ("a_c1", got_q)],
                    [k_l2, k_b1, ("a_s1", got_s)], [k_l2, k_b1, ("a_s1", got_s)]))


    kw = [op("s", lambda: S.activation(T.w3[:, 256 * i:256 * i + 256], T.vl[:].indirect(T.dup[:, 16 * i:16 * i + 16]),
                                       AF.Relu, bias=T.ft[:, 3 * me:3 * me + 1], scale=float(U)), vl, k_ft, k_dup)
          for i in range(2)]
    k_b2 = op("s", lambda: S.activation(T.land2s[:, L2W - 48:L2W], T.land1s[:].indirect(la), AF.Copy))
    for i in range(2):
        k = op("v", lambda: V.transpose(T.y3[:, 256 * i:256 * i + 256], T.w3[:, 256 * i:256 * i + 256]), kw[i])
        if i == 0:
            k_a2 = op("v", lambda: V.tensor_copy(T.land2q[:, L2W - 48:L2W].bitcast(u32),
                                                 T.land1q[:].bitcast(u32).indirect(la)))
        else:
            k_wq = op("v", lambda: V.quantize_mx(T.wq[:], T.ws[:], T.wt[:]), wl)
        k = op("v", lambda: V.tensor_tensor_scan(T.fo[:, 64 * i:64 * i + 64], T.rst[:, 0:C:4],
                                                 T.y3[:, 256 * i:256 * i + 256:4], 0.0, A.mult, A.add), k)
    z = T.fo[:, 7:128:8]
    op("v", lambda: V.tensor_scalar(T.hz[:, 0:64:4], z, 1.0 / 7, R23, A.mult, A.add), k)
    op("v", lambda: V.tensor_copy(T.hz[:, 2:64:4], z))
    k = op("v", lambda: V.tensor_scalar(T.hz[:, 3:64:4], z, 1.0 / (7 * U), R23, A.mult, A.add))
    k = op("v", lambda: V.tensor_tensor_scan(T.ho[:], T.hm[:], T.hz[:], 0.0, A.mult, A.add), k, k_hm)
    k_l3 = op("v", lambda: V.tensor_scalar(T.lst3[:], T.ho[:, 3:64:4], L2 + 3.0 * P2 - 1 - R23, None, A.add), k)

    c2, s2 = ("a_c2", got_q), ("a_s2", got_s)
    cols = [slice(128 * i, 128 * i + 128) for i in range(2)]
    lst = [T.lst3[:, 8 * i:8 * i + 8] for i in range(2)]
    kq = [op("v", lambda: V.tensor_copy(T.fq[:, cols[i]].bitcast(u32), T.land2q[:].bitcast(u32).indirect(lst[i])),
             k_l3, k_a2, c2) for i in range(2)]
    ks = [op("s", lambda: S.activation(T.fs[:, cols[i]], T.land2s[:].indirect(lst[i]), AF.Copy), k_l3, k_b2, s2)
          for i in range(2)]
    mm = [op("t", lambda: g.tensor.matmul_mx(T.ps[:, 512 * i:512 * i + 128], T.wq[:], T.ws[:], T.fq[:, cols[i]],
                                             T.fs[:, cols[i]], True, True), kq[i], ks[i], k_wq) for i in range(2)]
    k0 = op("v", lambda: V.tensor_copy(T.ys[:, 0:128], T.ps[:, 0:128]), mm[0])
    k1 = op("s", lambda: S.activation(T.ys[:, 128:256], T.ps[:, 512:640], AF.Copy), mm[1])
    y0 = dma("y", "d_y0", T.y[:, 0:128], T.ys[:, 0:128], k0)
    y1 = dma("s", "d_y1", T.y[:, 128:256], T.ys[:, 128:256], k1)

    wait("g", ("sent", sent[0]))
    wait("y", y0, y1, *[(s, count[s]) for s in ("ev", "es", "eg", "et")])
